import numpy as np
import ml_dtypes


def mxq(x, axis, fmt="e4m3"):
    dtype, down = {"e4m3": (ml_dtypes.float8_e4m3fn, 7), "e5m2": (ml_dtypes.float8_e5m2, 14)}[fmt]
    v = np.moveaxis(np.asarray(x, np.float32).astype(ml_dtypes.bfloat16).astype(np.float64), axis, -1)
    blocks = v.reshape(v.shape[:-1] + (-1, 32))
    amax = np.abs(blocks).max(-1, keepdims=True)
    byte = np.maximum(np.where(amax > 0, np.frexp(amax)[1] - 1 + 127, 0) - down, 1)
    scale = np.exp2(byte - 127.0)
    codes = (blocks / scale).astype(np.float32).astype(dtype).astype(np.float64)
    return np.moveaxis((codes * scale).reshape(v.shape), -1, axis)


WIDE = False


def mx_kscale(k):
    if not WIDE:
        return np.ones(k)
    levels = np.array([10, -10, 5, -5, 0])
    if k % 512:
        return np.exp2(np.random.permutation(np.resize(levels, k // 32))).repeat(32)
    a = np.empty((k // 512, 16))
    for p in range(k // 512):
        a[p, :8] = np.random.permutation(np.resize(levels, 8))
        for g in range(8):
            far = levels[np.abs(levels - a[p, g]) >= 10]
            a[p, g + 8] = far[np.random.randint(len(far))]
    return np.exp2(a.ravel()).repeat(32)


def f64(x):
    return np.asarray(x).astype(np.float64)


def striped(idx):
    return np.tile(idx.reshape(-1, 16).T, (8, 1)).astype(np.uint16)


def unstriped(offs):
    return offs[:16].T.reshape(-1).astype(np.int64)


E2M1 = np.array([0.0, 0.5, 1.0, 1.5, 2.0, 3.0, 4.0, 6.0, -0.0, -0.5, -1.0, -1.5, -2.0, -3.0, -4.0, -6.0])


def pack_weight(w, fmt):
    k, n = w.shape
    w = f64(np.asarray(w, np.float32).astype(ml_dtypes.bfloat16)).reshape(k // 32, 32, n)
    amax = np.abs(w).max(1)
    if fmt == "e4m3":
        byte = np.frexp(amax)[1] - 1 + 127 - 7
    else:
        mant, ex = np.frexp(amax / 6.0)
        byte = np.where(mant > 0.5, ex, ex - 1) + 127
    byte = np.clip(np.where(amax > 0, byte, 1), 1, 254)
    scaled = (w * np.exp2(127.0 - byte)[:, None, :]).reshape(k, n).astype(np.float32)
    by_word = np.ascontiguousarray(scaled.reshape(k // 512, 128, 4, n).transpose(0, 1, 3, 2))
    if fmt == "e4m3":
        words = by_word.astype(ml_dtypes.float8_e4m3fn).view(np.uint8)
    else:
        c = by_word.astype(ml_dtypes.float4_e2m1fn).view(np.uint8) & 0xF
        words = (c[..., 0::2] | (c[..., 1::2] << 4)).reshape(k // 512, 128, 2 * n)
    return np.ascontiguousarray(words), np.ascontiguousarray(byte.astype(np.uint8).reshape(k // 512, 16, n))


def unpack_weight(words, scales, fmt):
    g, _, n = scales.shape
    words = np.ascontiguousarray(words).reshape(g, 128, n, -1)
    if fmt == "e4m3":
        vals = words.view(ml_dtypes.float8_e4m3fn).astype(np.float64)
    else:
        nib = np.empty((g, 128, n, 4), np.uint8)
        nib[..., 0::2] = words & 0xF
        nib[..., 1::2] = words >> 4
        vals = E2M1[nib]
    vals = vals * np.repeat(np.exp2(scales.astype(np.float64) - 127.0), 8, axis=1)[..., None]
    return vals.transpose(0, 1, 3, 2).reshape(g * 512, n)


def gelu(v):
    return 0.5 * v * (1.0 + np.tanh(np.sqrt(2.0 / np.pi) * (v + 0.044715 * v**3)))


def striped8(idx):
    return np.concatenate([v.reshape(-1, 16).T for v in idx]).astype(np.uint16)


def unstriped8(offs):
    return np.stack([offs[16 * g:16 * g + 16].T.reshape(-1) for g in range(8)]).astype(np.int64)


def heads(h, wgt, idx8):
    r = np.arange(h.shape[0])
    return wgt[r // 4 % 128] * h[r[:, None], idx8[r % 512 // 64]]


def put_heads(h, wgs, idx8, t2):
    r = np.arange(h.shape[0])
    page = np.zeros((h.shape[0], t2))
    page[r[:, None], idx8[r % 512 // 64]] = wgs[r // 4 % 128] * h
    return page


K, H, N, T, S, P, T2 = 1024, 1024, 384, 4096, 1024, 1024, 2048

def setup_inputs():
    n = np.random.standard_normal
    s = mx_kscale(K)[:, None]
    u = mx_kscale(H)[:, None]
    d = {}
    d["tab_words"], d["tab_scales"] = pack_weight(n((K, T)) * s, "e4m3")
    d["offs"] = striped(np.random.permutation(T)[:S])
    d["offs2"] = striped8(np.stack([np.random.permutation(T2)[:S] for _ in range(8)]))
    d["offs3"] = striped8(np.stack([np.random.permutation(T2)[:P] for _ in range(8)]))
    d["w4_words"], d["w4_scales"] = pack_weight(0.6 * n((K, H)) / s / K ** 0.5, "e2m1")
    d["wang"] = (0.3 * n((K, H)) / s / K ** 0.5).astype(np.float32)
    d["tilt"] = np.random.uniform(-1.5, 1.5, H).astype(np.float32)
    d["gain"] = (np.exp(0.3 * n(H)) * u[:, 0]).astype(np.float32)
    d["wgs"] = np.repeat(np.random.uniform(0.5, 2.0, (8, S)), 16, axis=0).astype(np.float32)
    d["wgt"] = np.repeat(np.random.uniform(0.5, 2.0, (8, P)), 16, axis=0).astype(np.float32)
    d["execm"] = (0.8 * n((H, P)) * u).astype(np.float32)
    d["wform"] = (n((H, N)) / u / H ** 0.5).astype(np.float32)
    return d

def reference(tab_words, tab_scales, offs, offs2, offs3, w4_words, w4_scales, wang, tilt, gain, wgs, wgt, execm, wform):
    v = unpack_weight(tab_words, tab_scales, "e4m3")[:, unstriped(offs)]
    a = unpack_weight(w4_words, w4_scales, "e2m1").T @ v
    b = (mxq(f64(wang), 0, "e4m3").T @ v) + f64(tilt)[:, None]
    h = (a + np.sin(b) - np.cos(b)) * f64(gain)[:, None]
    page = put_heads(h, f64(wgs), unstriped8(offs2), T2)
    x = heads(page, f64(wgt), unstriped8(offs3))
    z = x - f64(execm)
    return mxq(f64(wform), 0, "e4m3").T @ mxq(z, 0, "e4m3")

@@ -1,0 +1,425 @@
+import math
+from contextlib import ExitStack
+
+import concourse.mybir as mybir
+from concourse.masks import make_identity
+
+K, H, N, T, S, M, T2 = 1024, 1024, 384, 4096, 1024, 1024, 2048
+FLOPS = 2 * (2 * K * H * S + H * N * M)
+
+F32 = mybir.dt.float32
+BF16 = mybir.dt.bfloat16
+I32 = mybir.dt.int32
+U32 = mybir.dt.uint32
+U16 = mybir.dt.uint16
+U8 = mybir.dt.uint8
+E4M3 = mybir.dt.float8_e4m3fn_x4
+E2M1 = mybir.dt.float4_e2m1fn_x4
+ALU = mybir.AluOpType
+ACT = mybir.ActivationFunctionType
+
+P = 128
+PACK = 4
+PASS = P * PACK
+HALF = 512
+BLOCKS = HALF // P
+CW, FB, TB = 3, 3, 3
+ROUNDER = 1.5 * 2.0 ** 23
+
+
+def tile_list_flight_shape_scores_kernel(
+    tc, tab_words, tab_scales, offs, offs2, offs3, w4_words, w4_scales,
+    wang, tilt, gain, wgs, wgt, execm, wform, out,
+):
+    nc = tc.nc
+    with ExitStack() as ctx:
+        lists = ctx.enter_context(tc.tile_pool(name="lists", bufs=1))
+        keep = ctx.enter_context(tc.tile_pool(name="keep", bufs=1))
+        ring = ctx.enter_context(tc.tile_pool(name="ring", bufs=2))
+        psum = ctx.enter_context(tc.psum_pool(name="psum", bufs=2))
+
+        pick = lists.tile([P, S // 16], U16, name="pick")
+        put = lists.tile([P, S // 16], U16, name="put")
+        read = lists.tile([P, M // 16], U16, name="read")
+
+        def entries(offsets, lo, width):
+            return offsets[:, lo // 16 : (lo + width) // 16]
+
+        tab_planes = keep.tile([P, 2, T], U8, name="tab_planes", align_bytes=64)
+        w4_planes = keep.tile([P, 2, H], U8, name="w4_planes", align_bytes=64)
+        nc.vector.memset(tab_planes[:, 0, :].bitcast(I32), 0)
+        nc.gpsimd.memset(tab_planes[:, 1, :].bitcast(I32), 0)
+        nc.gpsimd.memset(w4_planes[:].bitcast(I32), 0)
+        pages = []
+        for g in range(2):
+            page = keep.tile([P, T2], F32, name="page%d" % g)
+            nc.vector.memset(page[:], 0.0)
+            pages.append(page)
+        warm = keep.tile([P, 1], F32, name="warm")
+        nc.scalar.activation(warm[:], pages[0][:, 0:1], ACT.Sin)
+
+        table = []
+
+        def load_table(a):
+            words = ring.tile([P, T], I32, name="table", tag="wide")
+            nc.sync.dma_start(words[:], tab_words[a].rearrange("p t i -> p (t i)").bitcast(I32))
+            table.append(words)
+
+        def load_wang(b, a):
+            raw = ring.tile([P, PACK, PASS], F32, name="wang_raw", tag="raw", bufs=3)
+            rows = wang[a * PASS : (a + 1) * PASS, b * PASS : (b + 1) * PASS]
+            nc.sync.dma_start(raw[:], rows.rearrange("(p j) c -> p j c", j=PACK))
+            return raw
+
+        wang_raw = {(0, 0): load_wang(0, 0)}
+        nc.sync.dma_start(pick[:], offs)
+        wang_raw[0, 1] = load_wang(0, 1)
+        for q in range(4):
+            nc.sync.dma_start(
+                tab_planes[32 * q : 32 * q + 4].bitcast(I32),
+                tab_scales[:, 4 * q : 4 * q + 4, :].rearrange("a r t -> r a t").bitcast(I32),
+            )
+        load_table(0)
+        w4 = {}
+
+        def load_w4(b):
+            w4[b] = keep.tile([P, 2, 2 * PASS], U8, name="w4_%d" % b, align_bytes=64)
+            nc.sync.dma_start(
+                w4[b][:].bitcast(I32),
+                w4_words[:, :, 2 * b * PASS : 2 * (b + 1) * PASS].rearrange("a p c -> p a c").bitcast(I32),
+            )
+
+        load_w4(0)
+        load_table(1)
+        for q in range(4):
+            nc.gpsimd.dma_start(
+                w4_planes[32 * q : 32 * q + 4].bitcast(I32),
+                w4_scales[:, 4 * q : 4 * q + 4, :].rearrange("a r c -> r a c").bitcast(I32),
+            )
+        row_tilt = keep.tile([P, 2, PACK], F32, name="row_tilt")
+        row_gain = keep.tile([P, 2, PACK], F32, name="row_gain")
+        nc.gpsimd.dma_start(row_tilt[:], tilt.rearrange("(b p i) -> p b i", b=2, i=PACK))
+        nc.gpsimd.dma_start(row_gain[:], gain.rearrange("(b p i) -> p b i", b=2, i=PACK))
+        ident = keep.tile([P, P], F32, name="ident")
+        make_identity(nc, ident[:])
+
+        nc.sync.dma_start(put[:], offs2)
+        put_weight = keep.tile([P, S], F32, name="put_weight")
+        nc.sync.dma_start(put_weight[:], wgs)
+        nc.sync.dma_start(read[:], offs3)
+        read_weight = keep.tile([P, M], F32, name="read_weight")
+        nc.sync.dma_start(read_weight[:], wgt)
+        load_w4(1)
+
+        v_scales, v_words = {}, {}
+
+        def pick_columns():
+            for a in range(2):
+                plane = keep.tile([P, S], U8, name="v_scales%d" % a, align_bytes=64)
+                nc.vector.tensor_copy(plane[:], tab_planes[:, a, :].indirect(pick[:]))
+                for h in range(2):
+                    v_scales[a, h] = plane[:, h * HALF : (h + 1) * HALF]
+            for a in range(2):
+                for h in range(2):
+                    got = keep.tile([P, HALF], U32, name="v_words%d%d" % (a, h), align_bytes=64)
+                    nc.vector.tensor_copy(got[:], table[a][:].bitcast(U32).indirect(entries(pick, h * HALF, HALF)))
+                    v_words[a, h] = got
+
+        turns_bias = keep.tile([P, 2 * PACK], F32, name="turns_bias")
+        nc.vector.tensor_scalar(
+            turns_bias[:], row_tilt[:].rearrange("p b i -> p (b i)"),
+            -math.pi / 4, 1.0 / (2 * math.pi), ALU.add, ALU.mult,
+        )
+        gain_root2 = keep.tile([P, 2 * PACK], F32, name="gain_root2")
+        nc.vector.tensor_scalar(
+            gain_root2[:], row_gain[:].rearrange("p b i -> p (b i)"),
+            math.sqrt(2.0), None, ALU.mult,
+        )
+
+        wang_codes, wang_scales, wang_grouped = {}, {}, {}
+
+        def cast_wang(b, a, shares):
+            grouped = ring.tile([P, PASS * PACK], BF16, name="wang_grouped", tag="grouped", align_bytes=64)
+            dst = grouped[:].rearrange("p (t m j) -> p m j t", t=PACK, j=PACK)
+            src = wang_raw[b, a][:].rearrange("p j (m t) -> p m j t", t=PACK)
+            for engine_copy, lo, hi in shares:
+                engine_copy(dst[:, lo:hi], src[:, lo:hi])
+            wang_grouped[b, a] = grouped
+
+        def quantize_wang(b, a, cuts):
+            codes = keep.tile([P, PASS], U32, name="wang_codes%d%d" % (b, a), align_bytes=64)
+            scales = keep.tile([P, PASS], U8, name="wang_scales%d%d" % (b, a), align_bytes=64)
+            for lo, hi in cuts:
+                nc.vector.quantize_mx(
+                    out=codes[:, lo:hi].bitcast(E4M3), scales=scales[:, lo:hi],
+                    in_=wang_grouped[b, a][:, PACK * lo : PACK * hi],
+                )
+            wang_codes[b, a], wang_scales[b, a] = codes, scales
+
+        plain = {}
+
+        def plain_part(b, h, jb, on_vector=False):
+            if jb == 0:
+                plain[b, h] = ring.tile([P, BLOCKS, PACK, P], F32, name="plain", bufs=3)
+            bank = psum.tile([P, PASS], F32, name="plain_bank")
+            cols = slice(jb * P, (jb + 1) * P)
+            for a in range(2):
+                nc.tensor.matmul_mx(
+                    out=bank[:],
+                    lhsT=v_words[a, h][:, cols].bitcast(E4M3),
+                    lhsT_scale=v_scales[a, h][:, cols],
+                    rhs=w4[b][:, a, :].bitcast(E2M1),
+                    rhs_scale=w4_planes[:, a, b * PASS : (b + 1) * PASS],
+                    start=(a == 0), stop=(a == 1),
+                )
+            dealt = bank[:].rearrange("j (p i) -> j i p", i=PACK)
+            if on_vector:
+                nc.vector.tensor_scalar(plain[b, h][:, jb], dealt, 1.0 / math.sqrt(2.0), None, ALU.mult)
+            else:
+                nc.scalar.activation(plain[b, h][:, jb], dealt, ACT.Copy, scale=1.0 / math.sqrt(2.0))
+
+        for a in range(2):
+            cast_wang(0, a, [(nc.scalar.copy, 0, P)])
+            quantize_wang(0, a, [(0, PASS)])
+        pick_columns()
+
+        units = [(0, 0, 256), (0, 256, 256), (1, 0, HALF), (0, HALF, HALF), (1, HALF, HALF)]
+        units.extend((2 * pair + e, h * HALF, HALF) for pair in range(1, 4) for h in range(2) for e in range(2))
+        turns, whole, less, sines, feats, angle_banks, frac_banks, feat_banks = {}, {}, {}, {}, {}, {}, {}, {}
+
+        def angle_matmul(n):
+            s, lo, width = units[n]
+            b, i = divmod(s, PACK)
+            h, at = divmod(lo, HALF)
+            bank = psum.tile([P, HALF], F32, name="angle_bank")
+            for a in range(2):
+                nc.tensor.matmul_mx(
+                    out=bank[:, :width],
+                    lhsT=wang_codes[b, a][:, i * P : (i + 1) * P].bitcast(E4M3),
+                    lhsT_scale=wang_scales[b, a][:, i * P : (i + 1) * P],
+                    rhs=v_words[a, h][:, at : at + width].bitcast(E4M3),
+                    rhs_scale=v_scales[a, h][:, at : at + width],
+                    start=(a == 0), stop=(a == 1),
+                )
+            angle_banks[n] = bank
+
+        def to_turns(n):
+            s, lo, width = units[n]
+            turns[n] = ring.tile([P, HALF], F32, name="turns", bufs=TB)
+            nc.scalar.activation(
+                turns[n][:, :width], angle_banks[n][:, :width], ACT.Identity,
+                bias=turns_bias[:, s : s + 1], scale=1.0 / (2 * math.pi),
+            )
+
+        def to_whole(n):
+            width = units[n][2]
+            whole[n] = ring.tile([P, HALF], U32, name="whole")
+            nc.scalar.activation(whole[n][:, :width], turns[n][:, :width], ACT.Copy, bias=ROUNDER, scale=1.0)
+
+        def to_less(n):
+            width = units[n][2]
+            less[n] = ring.tile([P, HALF], F32, name="less")
+            nc.scalar.activation(less[n][:, :width], whole[n][:, :width], ACT.Copy, bias=ROUNDER, scale=-1.0)
+
+        def add_turned(bank, width, first, second):
+            for jb in range(width // P):
+                cols = slice(jb * P, (jb + 1) * P)
+                nc.tensor.matmul(bank[:, cols], first(jb), ident[:], is_transpose=True, start=True, stop=False)
+                nc.tensor.matmul(bank[:, cols], second(jb), ident[:], is_transpose=True, start=False, stop=True)
+
+        def fraction(n):
+            tag = "plain_bank" if n > 10 and n % 2 else "frac_bank"
+            bank = psum.tile([P, HALF], F32, name="frac_bank", tag=tag)
+            add_turned(
+                bank, units[n][2],
+                lambda jb: turns[n][:, jb * P : (jb + 1) * P],
+                lambda jb: less[n][:, jb * P : (jb + 1) * P],
+            )
+            frac_banks[n] = bank
+
+        def sine(n):
+            width = units[n][2]
+            sines[n] = ring.tile([P, HALF], F32, name="sines")
+            nc.scalar.activation(sines[n][:, :width], frac_banks[n][:, :width], ACT.Sin, scale=2 * math.pi)
+
+        def feature_sum(n):
+            s, lo, width = units[n]
+            b, i = divmod(s, PACK)
+            h, at = divmod(lo, HALF)
+            bank = psum.tile([P, HALF], F32, name="feat_bank")
+            add_turned(
+                bank, width,
+                lambda jb: plain[b, h][:, at // P + jb, i, :],
+                lambda jb: sines[n][:, jb * P : (jb + 1) * P],
+            )
+            feat_banks[n] = bank
+
+        def feature(n):
+            s, lo, width = units[n]
+            feats[n] = ring.tile([P, HALF], F32, name="feats", bufs=FB)
+            nc.scalar.activation(
+                feats[n][:, :width], feat_banks[n][:, :width], ACT.Copy, scale=gain_root2[:, s : s + 1]
+            )
+
+        def store_in_page(n):
+            s, lo, width = units[n]
+            nc.vector.tensor_tensor(
+                pages[s % 2][:].indirect(entries(put, lo, width)),
+                feats[n][:, :width], put_weight[:, lo : lo + width], ALU.mult,
+            )
+
+        routine, offsets_of, woven, z_codes, z_scales = {}, {}, {}, {}, {}
+
+        def read_page(s, lo, width):
+            b, i = divmod(s, PACK)
+            h, at = divmod(lo, HALF)
+            if i == 0:
+                routine[b, h] = ring.tile([P, PACK, HALF], F32, name="routine")
+            nc.vector.tensor_tensor(
+                routine[b, h][:, i, at : at + width],
+                pages[s % 2][:].indirect(entries(read, lo, width)),
+                read_weight[:, lo : lo + width], ALU.mult,
+            )
+
+        def load_execm(b):
+            offsets_of[b] = ring.tile([P, PACK, M], F32, name="exec_offsets", tag="wide")
+            nc.sync.dma_start(
+                offsets_of[b][:], execm[b * PASS : (b + 1) * PASS, :].rearrange("(p i) m -> p i m", i=PACK)
+            )
+
+        def subtract(b, lo, width):
+            h, at = divmod(lo, HALF)
+            woven[b, lo] = ring.tile([P, width * PACK], BF16, name="woven", align_bytes=64)
+            nc.vector.tensor_tensor(
+                woven[b, lo][:].rearrange("p (c w i) -> p c i w", w=4, i=PACK),
+                routine[b, h][:, :, at : at + width].rearrange("p i (c w) -> p c i w", w=4),
+                offsets_of[b][:, :, lo : lo + width].rearrange("p i (c w) -> p c i w", w=4),
+                ALU.subtract,
+            )
+
+        def quantize_z(b, lo, width):
+            if lo == 0:
+                z_codes[b] = keep.tile([P, M], U32, name="z_codes%d" % b, align_bytes=64)
+                z_scales[b] = keep.tile([P, M], U8, name="z_scales%d" % b, align_bytes=64)
+            nc.vector.quantize_mx(
+                out=z_codes[b][:, lo : lo + width].bitcast(E4M3), scales=z_scales[b][:, lo : lo + width],
+                in_=woven[b, lo][:],
+            )
+
+        form_grouped = keep.tile([P, 2, N, PACK], BF16, name="form_grouped", align_bytes=64)
+        form_codes = keep.tile([P, 2 * N], U32, name="form_codes", align_bytes=64)
+        form_scales = keep.tile([P, 2 * N], U8, name="form_scales", align_bytes=64)
+        form_raw = {}
+
+        def load_form(b):
+            form_raw[b] = ring.tile([P, PACK, N], F32, name="form_raw", tag="raw", bufs=3)
+            nc.sync.dma_start(
+                form_raw[b][:], wform[b * PASS : (b + 1) * PASS, :].rearrange("(p i) n -> p i n", i=PACK)
+            )
+
+        def cast_form(b):
+            for nt in range(3):
+                cols = slice(nt * P, (nt + 1) * P)
+                nc.scalar.copy(
+                    form_grouped[:, b, cols].rearrange("p (c w) i -> p c i w", w=4),
+                    form_raw[b][:, :, cols].rearrange("p i (c w) -> p c i w", w=4),
+                )
+
+        def quantize_form():
+            flat = form_grouped[:].rearrange("p b n i -> p (b n i)")
+            for lo, hi in ((0, 512), (512, 768)):
+                nc.vector.quantize_mx(
+                    out=form_codes[:, lo:hi].bitcast(E4M3), scales=form_scales[:, lo:hi],
+                    in_=flat[:, PACK * lo : PACK * hi],
+                )
+
+        score_banks = {}
+        free_tags = ["angle_bank", "angle_bank", "frac_bank", "frac_bank", "plain_bank", "plain_bank",
+                     "feat_bank", "feat_bank", "angle_bank"]
+
+        def score_pass(b, c, nt):
+            lo, width = chunks[1][c]
+            if b == 0:
+                score_banks[c, nt] = psum.tile([P, HALF], F32, name="score_bank", tag=free_tags[3 * c + nt])
+            cols = slice(b * N + nt * P, b * N + (nt + 1) * P)
+            nc.tensor.matmul_mx(
+                out=score_banks[c, nt][:, :width],
+                lhsT=form_codes[:, cols].bitcast(E4M3), lhsT_scale=form_scales[:, cols],
+                rhs=z_codes[b][:, lo : lo + width].bitcast(E4M3), rhs_scale=z_scales[b][:, lo : lo + width],
+                start=(b == 0), stop=(b == 1),
+            )
+
+        def store_scores(c, engine_copies):
+            lo, width = chunks[1][c]
+            scores = ring.tile([P, 3, width], F32, name="scores", tag="raw", bufs=3)
+            for nt in range(3):
+                score_pass(1, c, nt)
+                engine_copies[nt](scores[:, nt, :], score_banks[c, nt][:, :width])
+            nc.sync.dma_start(out[:, lo : lo + width].rearrange("(t p) m -> p t m", p=P), scores[:])
+
+        load_execm(0)
+        for a in range(2):
+            wang_raw[1, a] = load_wang(1, a)
+        load_form(0)
+        load_form(1)
+        load_execm(1)
+
+        halves = [(0, HALF), (HALF, HALF)]
+        chunks = [halves, [(0, HALF), (HALF, 256), (HALF + 256, 256)]]
+
+        extra = {}
+
+        def at(step, job, *args):
+            extra.setdefault(step, []).append((job, args))
+
+        before_sum = {3: [(plain_part, (0, 1, jb)) for jb in range(BLOCKS)]}
+        for jb in range(BLOCKS):
+            at(5 + jb, plain_part, 1, 0, jb)
+            at(9 + jb // 2, plain_part, 1, 1, jb)
+        for a in range(2):
+            at(CW + a, cast_wang, 1, a, [(nc.scalar.copy, 32 * c, 32 * c + 32) for c in range(4)])
+            at(CW + a, quantize_wang, 1, a, [(0, PASS)])
+            at(10 + a, cast_form, a)
+        at(11, quantize_form)
+        for s in range(7):
+            last = 4 * (s // 2) + 3 + s % 2
+            for h in range(2):
+                at(last, read_page, s, h * HALF, HALF)
+        for lo, width in halves:
+            at(8, subtract, 0, lo, width)
+        for lo, width in halves:
+            at(8, quantize_z, 0, lo, width)
+
+        count = len(units)
+        for n in range(count):
+            angle_matmul(n)
+            if n == 0:
+                for jb in range(BLOCKS):
+                    plain_part(0, 0, jb, True)
+            to_turns(n)
+            to_whole(n)
+            to_less(n)
+            fraction(n)
+            sine(n)
+            for job, args in before_sum.get(n, []):
+                job(*args)
+            feature_sum(n)
+            feature(n)
+            store_in_page(n)
+            for job, args in extra.get(n, []):
+                job(*args)
+
+        for c in range(3):
+            for nt in range(3):
+                if 3 * c + nt < 8:
+                    score_pass(0, c, nt)
+        for c, (lo, width) in enumerate(chunks[1]):
+            read_page(7, lo, width)
+            if c > 0:
+                quantize_z(1, *chunks[1][c - 1])
+            subtract(1, lo, width)
+            if c > 0:
+                store_scores(c - 1, [nc.scalar.copy] * 3)
+        score_pass(0, 2, 2)
+        quantize_z(1, *chunks[1][2])
+        store_scores(2, [nc.scalar.copy, nc.vector.tensor_copy, nc.scalar.copy])

@@ -23,7 +23,7 @@ PACK = 4
 PASS = P * PACK
 HALF = 512
 BLOCKS = HALF // P
-CW, FB, TB = 3, 3, 3
+CW, FB, TB, ZS = 1, 3, 3, 10
 ROUNDER = 1.5 * 2.0 ** 23
 
 
@@ -45,7 +45,7 @@ def tile_list_flight_shape_scores_kernel(
         def entries(offsets, lo, width):
             return offsets[:, lo // 16 : (lo + width) // 16]
 
-        tab_planes = keep.tile([P, 2, T], U8, name="tab_planes", align_bytes=64)
+        tab_planes = ring.tile([P, 2, T], U8, name="tab_planes", tag="routine")
         w4_planes = keep.tile([P, 2, H], U8, name="w4_planes", align_bytes=64)
         nc.vector.memset(tab_planes[:, 0, :].bitcast(I32), 0)
         nc.gpsimd.memset(tab_planes[:, 1, :].bitcast(I32), 0)
@@ -92,23 +92,25 @@ def tile_list_flight_shape_scores_kernel(
         load_w4(0)
         load_table(1)
         for q in range(4):
-            nc.gpsimd.dma_start(
+            nc.sync.dma_start(
                 w4_planes[32 * q : 32 * q + 4].bitcast(I32),
                 w4_scales[:, 4 * q : 4 * q + 4, :].rearrange("a r c -> r a c").bitcast(I32),
             )
         row_tilt = keep.tile([P, 2, PACK], F32, name="row_tilt")
         row_gain = keep.tile([P, 2, PACK], F32, name="row_gain")
-        nc.gpsimd.dma_start(row_tilt[:], tilt.rearrange("(b p i) -> p b i", b=2, i=PACK))
-        nc.gpsimd.dma_start(row_gain[:], gain.rearrange("(b p i) -> p b i", b=2, i=PACK))
+        nc.sync.dma_start(row_tilt[:], tilt.rearrange("(b p i) -> p b i", b=2, i=PACK))
+        nc.sync.dma_start(row_gain[:], gain.rearrange("(b p i) -> p b i", b=2, i=PACK))
         ident = keep.tile([P, P], F32, name="ident")
         make_identity(nc, ident[:])
 
         nc.sync.dma_start(put[:], offs2)
-        put_weight = keep.tile([P, S], F32, name="put_weight")
-        nc.sync.dma_start(put_weight[:], wgs)
-        nc.sync.dma_start(read[:], offs3)
         read_weight = keep.tile([P, M], F32, name="read_weight")
         nc.sync.dma_start(read_weight[:], wgt)
+        put_weight = keep.tile([P, S], F32, name="put_weight")
+        wang_raw[1, 0] = load_wang(1, 0)
+        nc.sync.dma_start(put_weight[:], wgs)
+        wang_raw[1, 1] = load_wang(1, 1)
+        nc.sync.dma_start(read[:], offs3)
         load_w4(1)
 
         v_scales, v_words = {}, {}
@@ -130,6 +132,8 @@ def tile_list_flight_shape_scores_kernel(
             turns_bias[:], row_tilt[:].rearrange("p b i -> p (b i)"),
             -math.pi / 4, 1.0 / (2 * math.pi), ALU.add, ALU.mult,
         )
+        minus_read_weight = keep.tile([P, M], F32, name="minus_read_weight")
+        nc.vector.tensor_scalar(minus_read_weight[:], read_weight[:], -1.0, None, ALU.mult)
         gain_root2 = keep.tile([P, 2 * PACK], F32, name="gain_root2")
         nc.vector.tensor_scalar(
             gain_root2[:], row_gain[:].rearrange("p b i -> p (b i)"),
@@ -228,7 +232,7 @@ def tile_list_flight_shape_scores_kernel(
                 nc.tensor.matmul(bank[:, cols], second(jb), ident[:], is_transpose=True, start=False, stop=True)
 
         def fraction(n):
-            tag = "plain_bank" if n > 10 and n % 2 else "frac_bank"
+            tag = "plain_bank" if n in (ZS - 1, ZS) else "frac_bank"
             bank = psum.tile([P, HALF], F32, name="frac_bank", tag=tag)
             add_turned(
                 bank, units[n][2],
@@ -272,13 +276,12 @@ def tile_list_flight_shape_scores_kernel(
 
         def read_page(s, lo, width):
             b, i = divmod(s, PACK)
-            h, at = divmod(lo, HALF)
             if i == 0:
-                routine[b, h] = ring.tile([P, PACK, HALF], F32, name="routine")
+                routine[b] = ring.tile([P, PACK, M], F32, name="routine")
             nc.vector.tensor_tensor(
-                routine[b, h][:, i, at : at + width],
+                routine[b][:, i, lo : lo + width],
                 pages[s % 2][:].indirect(entries(read, lo, width)),
-                read_weight[:, lo : lo + width], ALU.mult,
+                (minus_read_weight if b == 0 else read_weight)[:, lo : lo + width], ALU.mult,
             )
 
         def load_execm(b):
@@ -288,13 +291,46 @@ def tile_list_flight_shape_scores_kernel(
             )
 
         def subtract(b, lo, width):
-            h, at = divmod(lo, HALF)
-            woven[b, lo] = ring.tile([P, width * PACK], BF16, name="woven", align_bytes=64)
+            woven[b, lo] = ring.tile([P, width * PACK], BF16, name="woven", tag="grouped", align_bytes=64)
             nc.vector.tensor_tensor(
                 woven[b, lo][:].rearrange("p (c w i) -> p c i w", w=4, i=PACK),
-                routine[b, h][:, :, at : at + width].rearrange("p i (c w) -> p c i w", w=4),
+                routine[b][:, :, lo : lo + width].rearrange("p i (c w) -> p c i w", w=4),
                 offsets_of[b][:, :, lo : lo + width].rearrange("p i (c w) -> p c i w", w=4),
                 ALU.subtract,
+            )
+
+        turned_pairs = {}
+
+        def turned_difference(u, q):
+            bank = psum.tile([P, 2, 2 * P], F32, name="difference_bank", tag="plain_bank")
+            for e in range(2):
+                for k in range(2):
+                    cols = slice((2 * q + k) * P, (2 * q + k + 1) * P)
+                    into = bank[:, e, k * P : (k + 1) * P]
+                    nc.tensor.matmul(into, routine[0][:, 2 * u + e, cols], ident[:],
+                                     is_transpose=True, start=True, stop=False)
+                    nc.tensor.matmul(into, offsets_of[0][:, 2 * u + e, cols], ident[:],
+                                     is_transpose=True, start=False, stop=True)
+            turned_pairs[u, q] = ring.tile([P, 4 * P], BF16, name="turned_pairs", bufs=4)
+            nc.scalar.activation(
+                turned_pairs[u, q][:].rearrange("m (c w e) -> m c e w", w=4, e=2),
+                bank[:].rearrange("m e (c w) -> m c e w", w=4),
+                ACT.Copy, scale=-1.0,
+            )
+
+        def turn_back(q):
+            h, part = divmod(q, 2)
+            if part == 0:
+                woven[0, h * HALF] = ring.tile([P, HALF * PACK], BF16, name="woven", tag="grouped", align_bytes=64)
+            bank = psum.tile([P, 2, 2 * P], F32, name="words_bank", tag="plain_bank")
+            for u in range(2):
+                words = turned_pairs[u, q][:].bitcast(F32)
+                for k in range(2):
+                    nc.tensor.transpose(bank[:, u, k * P : (k + 1) * P], words[:, k * P : (k + 1) * P], ident[:])
+            nc.scalar.copy(
+                woven[0, h * HALF][:].bitcast(F32)[:, part * HALF : (part + 1) * HALF]
+                .rearrange("p (c w u) -> p c u w", w=4, u=2),
+                bank[:].rearrange("p u (c w) -> p c u w", w=4),
             )
 
         def quantize_z(b, lo, width):
@@ -335,37 +371,43 @@ def tile_list_flight_shape_scores_kernel(
 
         score_banks = {}
         free_tags = ["angle_bank", "angle_bank", "frac_bank", "frac_bank", "plain_bank", "plain_bank",
-                     "feat_bank", "feat_bank", "angle_bank"]
+                     "feat_bank", "feat_bank"]
 
-        def score_pass(b, c, nt):
-            lo, width = chunks[1][c]
-            if b == 0:
-                score_banks[c, nt] = psum.tile([P, HALF], F32, name="score_bank", tag=free_tags[3 * c + nt])
-            cols = slice(b * N + nt * P, b * N + (nt + 1) * P)
-            nc.tensor.matmul_mx(
-                out=score_banks[c, nt][:, :width],
-                lhsT=form_codes[:, cols].bitcast(E4M3), lhsT_scale=form_scales[:, cols],
-                rhs=z_codes[b][:, lo : lo + width].bitcast(E4M3), rhs_scale=z_scales[b][:, lo : lo + width],
-                start=(b == 0), stop=(b == 1),
-            )
-
-        def store_scores(c, engine_copies):
-            lo, width = chunks[1][c]
-            scores = ring.tile([P, 3, width], F32, name="scores", tag="raw", bufs=3)
+        def score_passes(b, c):
+            lo, width = chunks[c]
+            share = HALF // width
             for nt in range(3):
-                score_pass(1, c, nt)
-                engine_copies[nt](scores[:, nt, :], score_banks[c, nt][:, :width])
+                k, place = divmod(nt, share)
+                if b == 0 and place == 0:
+                    bank = psum.tile([P, HALF], F32, name="score_bank", tag=free_tags[len(score_banks)])
+                    score_banks[c, k] = bank
+                cols = slice(b * N + nt * P, b * N + (nt + 1) * P)
+                nc.tensor.matmul_mx(
+                    out=score_banks[c, k][:, place * width : (place + 1) * width],
+                    lhsT=form_codes[:, cols].bitcast(E4M3), lhsT_scale=form_scales[:, cols],
+                    rhs=z_codes[b][:, lo : lo + width].bitcast(E4M3), rhs_scale=z_scales[b][:, lo : lo + width],
+                    start=(b == 0 and place == 0), stop=(b == 1 and (nt == 2 or place == share - 1)),
+                )
+
+        def store_scores(c, engine_copy):
+            lo, width = chunks[c]
+            share = HALF // width
+            score_passes(1, c)
+            scores = ring.tile([P, 3, width], F32, name="scores", tag="raw" if c < 3 else "plain", bufs=3)
+            for first in range(0, 3, share):
+                last = min(first + share, 3)
+                engine_copy(
+                    scores[:, first:last, :].rearrange("p t m -> p (t m)"),
+                    score_banks[c, first // share][:, : (last - first) * width],
+                )
             nc.sync.dma_start(out[:, lo : lo + width].rearrange("(t p) m -> p t m", p=P), scores[:])
 
         load_execm(0)
-        for a in range(2):
-            wang_raw[1, a] = load_wang(1, a)
         load_form(0)
         load_form(1)
         load_execm(1)
 
-        halves = [(0, HALF), (HALF, HALF)]
-        chunks = [halves, [(0, HALF), (HALF, 256), (HALF + 256, 256)]]
+        chunks = [(0, 256), (256, 256), (512, 256), (768, P), (896, P)]
 
         extra = {}
 
@@ -377,28 +419,35 @@ def tile_list_flight_shape_scores_kernel(
             at(5 + jb, plain_part, 1, 0, jb)
             at(9 + jb // 2, plain_part, 1, 1, jb)
         for a in range(2):
-            at(CW + a, cast_wang, 1, a, [(nc.scalar.copy, 32 * c, 32 * c + 32) for c in range(4)])
+            at(CW + a, cast_wang, 1, a, [(nc.vector.tensor_copy, 64 * c, 64 * c + 64) for c in range(2)])
             at(CW + a, quantize_wang, 1, a, [(0, PASS)])
             at(10 + a, cast_form, a)
         at(11, quantize_form)
         for s in range(7):
             last = 4 * (s // 2) + 3 + s % 2
-            for h in range(2):
-                at(last, read_page, s, h * HALF, HALF)
-        for lo, width in halves:
-            at(8, subtract, 0, lo, width)
-        for lo, width in halves:
-            at(8, quantize_z, 0, lo, width)
+            at(last, read_page, s, 0, M)
+        for q in range(4):
+            at(ZS + q, turned_difference, 0, q)
+            at(ZS + q, turned_difference, 1, q)
+            at(ZS + q, turn_back, q)
+            if q % 2:
+                at(ZS + q, quantize_z, 0, q // 2 * HALF, HALF)
 
-        count = len(units)
-        for n in range(count):
+        def reduce_angle(n):
             angle_matmul(n)
-            if n == 0:
-                for jb in range(BLOCKS):
-                    plain_part(0, 0, jb, True)
             to_turns(n)
             to_whole(n)
             to_less(n)
+
+        AHEAD = 3
+        for n in range(AHEAD):
+            reduce_angle(n)
+        for jb in range(BLOCKS):
+            plain_part(0, 0, jb, True)
+        count = len(units)
+        for n in range(count):
+            if n >= AHEAD:
+                reduce_angle(n)
             fraction(n)
             sine(n)
             for job, args in before_sum.get(n, []):
@@ -409,17 +458,13 @@ def tile_list_flight_shape_scores_kernel(
             for job, args in extra.get(n, []):
                 job(*args)
 
-        for c in range(3):
-            for nt in range(3):
-                if 3 * c + nt < 8:
-                    score_pass(0, c, nt)
-        for c, (lo, width) in enumerate(chunks[1]):
+        for c in range(len(chunks)):
+            score_passes(0, c)
+        for c, (lo, width) in enumerate(chunks):
             read_page(7, lo, width)
             if c > 0:
-                quantize_z(1, *chunks[1][c - 1])
+                quantize_z(1, *chunks[c - 1])
+                store_scores(c - 1, nc.scalar.copy)
             subtract(1, lo, width)
-            if c > 0:
-                store_scores(c - 1, [nc.scalar.copy] * 3)
-        score_pass(0, 2, 2)
-        quantize_z(1, *chunks[1][2])
-        store_scores(2, [nc.scalar.copy, nc.vector.tensor_copy, nc.scalar.copy])
+        quantize_z(1, *chunks[-1])
+        store_scores(len(chunks) - 1, nc.vector.tensor_copy)

@@ -23,7 +23,7 @@ PACK = 4
 PASS = P * PACK
 HALF = 512
 BLOCKS = HALF // P
-CW, FB, TB, ZS = 1, 3, 3, 10
+CW, FB, TB = 1, 3, 3
 ROUNDER = 1.5 * 2.0 ** 23
 
 
@@ -71,15 +71,6 @@ def tile_list_flight_shape_scores_kernel(
             nc.sync.dma_start(raw[:], rows.rearrange("(p j) c -> p j c", j=PACK))
             return raw
 
-        wang_raw = {(0, 0): load_wang(0, 0)}
-        nc.sync.dma_start(pick[:], offs)
-        wang_raw[0, 1] = load_wang(0, 1)
-        for q in range(4):
-            nc.sync.dma_start(
-                tab_planes[32 * q : 32 * q + 4].bitcast(I32),
-                tab_scales[:, 4 * q : 4 * q + 4, :].rearrange("a r t -> r a t").bitcast(I32),
-            )
-        load_table(0)
         w4 = {}
 
         def load_w4(b):
@@ -89,29 +80,36 @@ def tile_list_flight_shape_scores_kernel(
                 w4_words[:, :, 2 * b * PASS : 2 * (b + 1) * PASS].rearrange("a p c -> p a c").bitcast(I32),
             )
 
-        load_w4(0)
-        load_table(1)
-        for q in range(4):
+        nc.sync.dma_start(pick[:], offs)
+        load_table(0)
+        for r in range(4):
             nc.sync.dma_start(
-                w4_planes[32 * q : 32 * q + 4].bitcast(I32),
-                w4_scales[:, 4 * q : 4 * q + 4, :].rearrange("a r c -> r a c").bitcast(I32),
+                tab_planes[r:P:32].bitcast(I32),
+                tab_scales[:, r:16:4, :].rearrange("a q t -> q a t").bitcast(I32),
             )
+        wang_raw = {(0, a): load_wang(0, a) for a in range(2)}
         row_tilt = keep.tile([P, 2, PACK], F32, name="row_tilt")
         row_gain = keep.tile([P, 2, PACK], F32, name="row_gain")
         nc.sync.dma_start(row_tilt[:], tilt.rearrange("(b p i) -> p b i", b=2, i=PACK))
         nc.sync.dma_start(row_gain[:], gain.rearrange("(b p i) -> p b i", b=2, i=PACK))
-        ident = keep.tile([P, P], F32, name="ident")
-        make_identity(nc, ident[:])
-
+        load_w4(0)
+        load_table(1)
+        for r in range(4):
+            nc.sync.dma_start(
+                w4_planes[r:P:32].bitcast(I32),
+                w4_scales[:, r:16:4, :].rearrange("a q c -> q a c").bitcast(I32),
+            )
+        put_weight = keep.tile([P, S], F32, name="put_weight")
+        nc.sync.dma_start(put_weight[:], wgs)
         nc.sync.dma_start(put[:], offs2)
+        for a in range(2):
+            wang_raw[1, a] = load_wang(1, a)
+        nc.sync.dma_start(read[:], offs3)
         read_weight = keep.tile([P, M], F32, name="read_weight")
         nc.sync.dma_start(read_weight[:], wgt)
-        put_weight = keep.tile([P, S], F32, name="put_weight")
-        wang_raw[1, 0] = load_wang(1, 0)
-        nc.sync.dma_start(put_weight[:], wgs)
-        wang_raw[1, 1] = load_wang(1, 1)
-        nc.sync.dma_start(read[:], offs3)
         load_w4(1)
+        ident = keep.tile([P, P], F32, name="ident")
+        make_identity(nc, ident[:])
 
         v_scales, v_words = {}, {}
 
@@ -132,8 +130,6 @@ def tile_list_flight_shape_scores_kernel(
             turns_bias[:], row_tilt[:].rearrange("p b i -> p (b i)"),
             -math.pi / 4, 1.0 / (2 * math.pi), ALU.add, ALU.mult,
         )
-        minus_read_weight = keep.tile([P, M], F32, name="minus_read_weight")
-        nc.vector.tensor_scalar(minus_read_weight[:], read_weight[:], -1.0, None, ALU.mult)
         gain_root2 = keep.tile([P, 2 * PACK], F32, name="gain_root2")
         nc.vector.tensor_scalar(
             gain_root2[:], row_gain[:].rearrange("p b i -> p (b i)"),
@@ -144,8 +140,8 @@ def tile_list_flight_shape_scores_kernel(
 
         def cast_wang(b, a, shares):
             grouped = ring.tile([P, PASS * PACK], BF16, name="wang_grouped", tag="grouped", align_bytes=64)
-            dst = grouped[:].rearrange("p (t m j) -> p m j t", t=PACK, j=PACK)
-            src = wang_raw[b, a][:].rearrange("p j (m t) -> p m j t", t=PACK)
+            dst = grouped[:].rearrange("p (t m j) -> p m t j", t=PACK, j=PACK)
+            src = wang_raw[b, a][:].rearrange("p j (m t) -> p m t j", t=PACK)
             for engine_copy, lo, hi in shares:
                 engine_copy(dst[:, lo:hi], src[:, lo:hi])
             wang_grouped[b, a] = grouped
@@ -232,7 +228,7 @@ def tile_list_flight_shape_scores_kernel(
                 nc.tensor.matmul(bank[:, cols], second(jb), ident[:], is_transpose=True, start=False, stop=True)
 
         def fraction(n):
-            tag = "plain_bank" if n in (ZS - 1, ZS) else "frac_bank"
+            tag = "plain_bank" if n > 10 and n % 2 else "frac_bank"
             bank = psum.tile([P, HALF], F32, name="frac_bank", tag=tag)
             add_turned(
                 bank, units[n][2],
@@ -281,7 +277,7 @@ def tile_list_flight_shape_scores_kernel(
             nc.vector.tensor_tensor(
                 routine[b][:, i, lo : lo + width],
                 pages[s % 2][:].indirect(entries(read, lo, width)),
-                (minus_read_weight if b == 0 else read_weight)[:, lo : lo + width], ALU.mult,
+                read_weight[:, lo : lo + width], ALU.mult,
             )
 
         def load_execm(b):
@@ -293,44 +289,10 @@ def tile_list_flight_shape_scores_kernel(
         def subtract(b, lo, width):
             woven[b, lo] = ring.tile([P, width * PACK], BF16, name="woven", tag="grouped", align_bytes=64)
             nc.vector.tensor_tensor(
-                woven[b, lo][:].rearrange("p (c w i) -> p c i w", w=4, i=PACK),
-                routine[b][:, :, lo : lo + width].rearrange("p i (c w) -> p c i w", w=4),
-                offsets_of[b][:, :, lo : lo + width].rearrange("p i (c w) -> p c i w", w=4),
+                woven[b, lo][:].rearrange("p (c w i) -> p c i w", w=2, i=PACK),
+                routine[b][:, :, lo : lo + width].rearrange("p i (c w) -> p c i w", w=2),
+                offsets_of[b][:, :, lo : lo + width].rearrange("p i (c w) -> p c i w", w=2),
                 ALU.subtract,
-            )
-
-        turned_pairs = {}
-
-        def turned_difference(u, q):
-            bank = psum.tile([P, 2, 2 * P], F32, name="difference_bank", tag="plain_bank")
-            for e in range(2):
-                for k in range(2):
-                    cols = slice((2 * q + k) * P, (2 * q + k + 1) * P)
-                    into = bank[:, e, k * P : (k + 1) * P]
-                    nc.tensor.matmul(into, routine[0][:, 2 * u + e, cols], ident[:],
-                                     is_transpose=True, start=True, stop=False)
-                    nc.tensor.matmul(into, offsets_of[0][:, 2 * u + e, cols], ident[:],
-                                     is_transpose=True, start=False, stop=True)
-            turned_pairs[u, q] = ring.tile([P, 4 * P], BF16, name="turned_pairs", bufs=4)
-            nc.scalar.activation(
-                turned_pairs[u, q][:].rearrange("m (c w e) -> m c e w", w=4, e=2),
-                bank[:].rearrange("m e (c w) -> m c e w", w=4),
-                ACT.Copy, scale=-1.0,
-            )
-
-        def turn_back(q):
-            h, part = divmod(q, 2)
-            if part == 0:
-                woven[0, h * HALF] = ring.tile([P, HALF * PACK], BF16, name="woven", tag="grouped", align_bytes=64)
-            bank = psum.tile([P, 2, 2 * P], F32, name="words_bank", tag="plain_bank")
-            for u in range(2):
-                words = turned_pairs[u, q][:].bitcast(F32)
-                for k in range(2):
-                    nc.tensor.transpose(bank[:, u, k * P : (k + 1) * P], words[:, k * P : (k + 1) * P], ident[:])
-            nc.scalar.copy(
-                woven[0, h * HALF][:].bitcast(F32)[:, part * HALF : (part + 1) * HALF]
-                .rearrange("p (c w u) -> p c u w", w=4, u=2),
-                bank[:].rearrange("p u (c w) -> p c u w", w=4),
             )
 
         def quantize_z(b, lo, width):
@@ -357,8 +319,8 @@ def tile_list_flight_shape_scores_kernel(
             for nt in range(3):
                 cols = slice(nt * P, (nt + 1) * P)
                 nc.scalar.copy(
-                    form_grouped[:, b, cols].rearrange("p (c w) i -> p c i w", w=4),
-                    form_raw[b][:, :, cols].rearrange("p i (c w) -> p c i w", w=4),
+                    form_grouped[:, b, cols].rearrange("p (c w) i -> p c i w", w=2),
+                    form_raw[b][:, :, cols].rearrange("p i (c w) -> p c i w", w=2),
                 )
 
         def quantize_form():
@@ -426,12 +388,10 @@ def tile_list_flight_shape_scores_kernel(
         for s in range(7):
             last = 4 * (s // 2) + 3 + s % 2
             at(last, read_page, s, 0, M)
-        for q in range(4):
-            at(ZS + q, turned_difference, 0, q)
-            at(ZS + q, turned_difference, 1, q)
-            at(ZS + q, turn_back, q)
-            if q % 2:
-                at(ZS + q, quantize_z, 0, q // 2 * HALF, HALF)
+        for h in range(2):
+            at(8, subtract, 0, h * HALF, HALF)
+        for h in range(2):
+            at(8, quantize_z, 0, h * HALF, HALF)
 
         def reduce_angle(n):
             angle_matmul(n)

@@ -23,7 +23,10 @@ PACK = 4
 PASS = P * PACK
 HALF = 512
 BLOCKS = HALF // P
-CW, FB, TB = 1, 3, 3
+CW, FB, TB = 3, 3, 3
+DIRECT = (0, 1, 2, 3)
+PB, P0, P1, CV = 2, 7, 9, 0
+FP = (11, 13, 15)
 ROUNDER = 1.5 * 2.0 ** 23
 
 
@@ -55,8 +58,11 @@ def tile_list_flight_shape_scores_kernel(
             page = keep.tile([P, T2], F32, name="page%d" % g)
             nc.vector.memset(page[:], 0.0)
             pages.append(page)
-        warm = keep.tile([P, 1], F32, name="warm")
-        nc.scalar.activation(warm[:], pages[0][:, 0:1], ACT.Sin)
+
+        one = keep.tile([P, 1], F32, name="one")
+        nc.gpsimd.memset(one[:], 1.0)
+        sine_eighth = keep.tile([P, 1], F32, name="sine_eighth")
+        nc.scalar.activation(sine_eighth[:], one[:], ACT.Sin, scale=math.pi / 4)
 
         table = []
 
@@ -126,14 +132,13 @@ def tile_list_flight_shape_scores_kernel(
                     v_words[a, h] = got
 
         turns_bias = keep.tile([P, 2 * PACK], F32, name="turns_bias")
-        nc.vector.tensor_scalar(
-            turns_bias[:], row_tilt[:].rearrange("p b i -> p (b i)"),
-            -math.pi / 4, 1.0 / (2 * math.pi), ALU.add, ALU.mult,
+        nc.scalar.activation(
+            turns_bias[:], row_tilt[:].rearrange("p b i -> p (b i)"), ACT.Copy,
+            bias=-0.125, scale=1.0 / (2 * math.pi),
         )
         gain_root2 = keep.tile([P, 2 * PACK], F32, name="gain_root2")
         nc.vector.tensor_scalar(
-            gain_root2[:], row_gain[:].rearrange("p b i -> p (b i)"),
-            math.sqrt(2.0), None, ALU.mult,
+            gain_root2[:], row_gain[:].rearrange("p b i -> p (b i)"), sine_eighth[:], 2.0, ALU.mult, ALU.mult
         )
 
         wang_codes, wang_scales, wang_grouped = {}, {}, {}
@@ -160,7 +165,7 @@ def tile_list_flight_shape_scores_kernel(
 
         def plain_part(b, h, jb, on_vector=False):
             if jb == 0:
-                plain[b, h] = ring.tile([P, BLOCKS, PACK, P], F32, name="plain", bufs=3)
+                plain[b, h] = ring.tile([P, BLOCKS, PACK, P], F32, name="plain", bufs=PB)
             bank = psum.tile([P, PASS], F32, name="plain_bank")
             cols = slice(jb * P, (jb + 1) * P)
             for a in range(2):
@@ -228,7 +233,7 @@ def tile_list_flight_shape_scores_kernel(
                 nc.tensor.matmul(bank[:, cols], second(jb), ident[:], is_transpose=True, start=False, stop=True)
 
         def fraction(n):
-            tag = "plain_bank" if n > 10 and n % 2 else "frac_bank"
+            tag = "plain_bank" if n in FP else "frac_bank"
             bank = psum.tile([P, HALF], F32, name="frac_bank", tag=tag)
             add_turned(
                 bank, units[n][2],
@@ -355,7 +360,7 @@ def tile_list_flight_shape_scores_kernel(
             lo, width = chunks[c]
             share = HALF // width
             score_passes(1, c)
-            scores = ring.tile([P, 3, width], F32, name="scores", tag="raw" if c < 3 else "plain", bufs=3)
+            scores = ring.tile([P, 3, width], F32, name="scores", tag="raw" if c < 3 else "plain", bufs=3 if c < 3 else PB)
             for first in range(0, 3, share):
                 last = min(first + share, 3)
                 engine_copy(
@@ -378,10 +383,10 @@ def tile_list_flight_shape_scores_kernel(
 
         before_sum = {3: [(plain_part, (0, 1, jb)) for jb in range(BLOCKS)]}
         for jb in range(BLOCKS):
-            at(5 + jb, plain_part, 1, 0, jb)
-            at(9 + jb // 2, plain_part, 1, 1, jb)
+            at(P0 + jb // 2, plain_part, 1, 0, jb)
+            at(P1 + jb // 2, plain_part, 1, 1, jb)
         for a in range(2):
-            at(CW + a, cast_wang, 1, a, [(nc.vector.tensor_copy, 64 * c, 64 * c + 64) for c in range(2)])
+            at(CW + a, cast_wang, 1, a, [(nc.vector.tensor_copy if CV else nc.scalar.copy, 32 * c, 32 * c + 32) for c in range(4)])
             at(CW + a, quantize_wang, 1, a, [(0, PASS)])
             at(10 + a, cast_form, a)
         at(11, quantize_form)
@@ -397,7 +402,37 @@ def tile_list_flight_shape_scores_kernel(
             angle_matmul(n)
             to_turns(n)
             to_whole(n)
-            to_less(n)
+            if n in DIRECT:
+                fraction_direct(n)
+            else:
+                to_less(n)
+
+        def fraction_direct(n):
+            width = units[n][2]
+            less[n] = ring.tile([P, HALF], F32, name="less")
+            nc.vector.scalar_tensor_tensor(
+                less[n][:, :width], whole[n][:, :width].bitcast(I32), ROUNDER, turns[n][:, :width],
+                ALU.subtract, ALU.subtract,
+            )
+
+        def feature_direct(n):
+            s, lo, width = units[n]
+            b, i = divmod(s, PACK)
+            h, at_col = divmod(lo, HALF)
+            sines[n] = ring.tile([P, HALF], F32, name="sines")
+            nc.scalar.activation(sines[n][:, :width], less[n][:, :width], ACT.Sin, scale=-2 * math.pi)
+            for job, args in before_sum.get(n, []):
+                job(*args)
+            bank = psum.tile([P, HALF], F32, name="feat_bank")
+            for jb in range(width // P):
+                nc.tensor.transpose(bank[:, jb * P : (jb + 1) * P], plain[b, h][:, at_col // P + jb, i, :], ident[:])
+            gained = ring.tile([P, HALF], F32, name="gained")
+            nc.scalar.activation(gained[:, :width], bank[:, :width], ACT.Copy, scale=gain_root2[:, s : s + 1])
+            feats[n] = ring.tile([P, HALF], F32, name="feats", bufs=FB)
+            nc.vector.scalar_tensor_tensor(
+                feats[n][:, :width], sines[n][:, :width], gain_root2[:, s : s + 1], gained[:, :width],
+                ALU.mult, ALU.add,
+            )
 
         AHEAD = 3
         for n in range(AHEAD):
@@ -408,12 +443,15 @@ def tile_list_flight_shape_scores_kernel(
         for n in range(count):
             if n >= AHEAD:
                 reduce_angle(n)
-            fraction(n)
-            sine(n)
-            for job, args in before_sum.get(n, []):
-                job(*args)
-            feature_sum(n)
-            feature(n)
+            if n in DIRECT:
+                feature_direct(n)
+            else:
+                fraction(n)
+                sine(n)
+                for job, args in before_sum.get(n, []):
+                    job(*args)
+                feature_sum(n)
+                feature(n)
             store_in_page(n)
             for job, args in extra.get(n, []):
                 job(*args)

@@ -22,12 +22,23 @@ P = 128
 PACK = 4
 PASS = P * PACK
 HALF = 512
+QUARTER = HALF // 2
 BLOCKS = HALF // P
-CW, FB, TB = 3, 3, 3
-DIRECT = (0, 1, 2, 3)
-PB, P0, P1, CV = 2, 7, 9, 0
-FP = (11, 13, 15)
+SLICES = H // P
+SCORE_TILES = N // P
 ROUNDER = 1.5 * 2.0 ** 23
+
+UNITS = [(0, 0, QUARTER), (0, QUARTER, QUARTER), (1, 0, HALF), (0, HALF, HALF), (1, HALF, HALF)] + [
+    (2 * pair + e, h * HALF, HALF) for pair in range(1, SLICES // 2) for h in range(2) for e in range(2)
+]
+LAST_UNIT = len(UNITS) - 1
+ANGLES_AHEAD = 3
+WANG_UNIT, FORM_UNIT = 3, 10
+CHUNKS = [(0, QUARTER), (QUARTER, QUARTER), (HALF, QUARTER), (HALF + QUARTER, P), (M - P, P)]
+
+
+def last_unit_where(wanted):
+    return max(n for n, unit in enumerate(UNITS) if wanted(*unit))
 
 
 def tile_list_flight_shape_scores_kernel(
@@ -58,26 +69,21 @@ def tile_list_flight_shape_scores_kernel(
             page = keep.tile([P, T2], F32, name="page%d" % g)
             nc.vector.memset(page[:], 0.0)
             pages.append(page)
-
         one = keep.tile([P, 1], F32, name="one")
         nc.gpsimd.memset(one[:], 1.0)
         sine_eighth = keep.tile([P, 1], F32, name="sine_eighth")
         nc.scalar.activation(sine_eighth[:], one[:], ACT.Sin, scale=math.pi / 4)
 
-        table = []
+        table, wang_raw, w4 = {}, {}, {}
 
         def load_table(a):
-            words = ring.tile([P, T], I32, name="table", tag="wide")
-            nc.sync.dma_start(words[:], tab_words[a].rearrange("p t i -> p (t i)").bitcast(I32))
-            table.append(words)
+            table[a] = ring.tile([P, T], I32, name="table", tag="wide")
+            nc.sync.dma_start(table[a][:], tab_words[a].rearrange("p t i -> p (t i)").bitcast(I32))
 
         def load_wang(b, a):
-            raw = ring.tile([P, PACK, PASS], F32, name="wang_raw", tag="raw", bufs=3)
+            wang_raw[b, a] = ring.tile([P, PACK, PASS], F32, name="wang_raw", tag="raw", bufs=3)
             rows = wang[a * PASS : (a + 1) * PASS, b * PASS : (b + 1) * PASS]
-            nc.sync.dma_start(raw[:], rows.rearrange("(p j) c -> p j c", j=PACK))
-            return raw
-
-        w4 = {}
+            nc.sync.dma_start(wang_raw[b, a][:], rows.rearrange("(p j) c -> p j c", j=PACK))
 
         def load_w4(b):
             w4[b] = keep.tile([P, 2, 2 * PASS], U8, name="w4_%d" % b, align_bytes=64)
@@ -86,30 +92,30 @@ def tile_list_flight_shape_scores_kernel(
                 w4_words[:, :, 2 * b * PASS : 2 * (b + 1) * PASS].rearrange("a p c -> p a c").bitcast(I32),
             )
 
+        def load_planes(planes, scale_rows):
+            for r in range(4):
+                nc.sync.dma_start(
+                    planes[r:P:32].bitcast(I32),
+                    scale_rows[:, r:16:4, :].rearrange("a q c -> q a c").bitcast(I32),
+                )
+
         nc.sync.dma_start(pick[:], offs)
         load_table(0)
-        for r in range(4):
-            nc.sync.dma_start(
-                tab_planes[r:P:32].bitcast(I32),
-                tab_scales[:, r:16:4, :].rearrange("a q t -> q a t").bitcast(I32),
-            )
-        wang_raw = {(0, a): load_wang(0, a) for a in range(2)}
+        load_planes(tab_planes, tab_scales)
+        for a in range(2):
+            load_wang(0, a)
         row_tilt = keep.tile([P, 2, PACK], F32, name="row_tilt")
         row_gain = keep.tile([P, 2, PACK], F32, name="row_gain")
         nc.sync.dma_start(row_tilt[:], tilt.rearrange("(b p i) -> p b i", b=2, i=PACK))
         nc.sync.dma_start(row_gain[:], gain.rearrange("(b p i) -> p b i", b=2, i=PACK))
         load_w4(0)
         load_table(1)
-        for r in range(4):
-            nc.sync.dma_start(
-                w4_planes[r:P:32].bitcast(I32),
-                w4_scales[:, r:16:4, :].rearrange("a q c -> q a c").bitcast(I32),
-            )
+        load_planes(w4_planes, w4_scales)
         put_weight = keep.tile([P, S], F32, name="put_weight")
         nc.sync.dma_start(put_weight[:], wgs)
         nc.sync.dma_start(put[:], offs2)
         for a in range(2):
-            wang_raw[1, a] = load_wang(1, a)
+            load_wang(1, a)
         nc.sync.dma_start(read[:], offs3)
         read_weight = keep.tile([P, M], F32, name="read_weight")
         nc.sync.dma_start(read_weight[:], wgt)
@@ -117,163 +123,129 @@ def tile_list_flight_shape_scores_kernel(
         ident = keep.tile([P, P], F32, name="ident")
         make_identity(nc, ident[:])
 
-        v_scales, v_words = {}, {}
-
-        def pick_columns():
-            for a in range(2):
-                plane = keep.tile([P, S], U8, name="v_scales%d" % a, align_bytes=64)
-                nc.vector.tensor_copy(plane[:], tab_planes[:, a, :].indirect(pick[:]))
-                for h in range(2):
-                    v_scales[a, h] = plane[:, h * HALF : (h + 1) * HALF]
-            for a in range(2):
-                for h in range(2):
-                    got = keep.tile([P, HALF], U32, name="v_words%d%d" % (a, h), align_bytes=64)
-                    nc.vector.tensor_copy(got[:], table[a][:].bitcast(U32).indirect(entries(pick, h * HALF, HALF)))
-                    v_words[a, h] = got
-
-        turns_bias = keep.tile([P, 2 * PACK], F32, name="turns_bias")
+        turns_bias = keep.tile([P, SLICES], F32, name="turns_bias")
         nc.scalar.activation(
             turns_bias[:], row_tilt[:].rearrange("p b i -> p (b i)"), ACT.Copy,
-            bias=-0.125, scale=1.0 / (2 * math.pi),
+            bias=-1.0 / 8, scale=1.0 / (2 * math.pi),
         )
-        gain_root2 = keep.tile([P, 2 * PACK], F32, name="gain_root2")
+        gain_root2 = keep.tile([P, SLICES], F32, name="gain_root2")
         nc.vector.tensor_scalar(
             gain_root2[:], row_gain[:].rearrange("p b i -> p (b i)"), sine_eighth[:], 2.0, ALU.mult, ALU.mult
         )
 
-        wang_codes, wang_scales, wang_grouped = {}, {}, {}
+        wang_codes, wang_scales = {}, {}
 
-        def cast_wang(b, a, shares):
-            grouped = ring.tile([P, PASS * PACK], BF16, name="wang_grouped", tag="grouped", align_bytes=64)
-            dst = grouped[:].rearrange("p (t m j) -> p m t j", t=PACK, j=PACK)
-            src = wang_raw[b, a][:].rearrange("p j (m t) -> p m t j", t=PACK)
-            for engine_copy, lo, hi in shares:
-                engine_copy(dst[:, lo:hi], src[:, lo:hi])
-            wang_grouped[b, a] = grouped
+        def quantize_wang(b, a, engine_copy, pieces):
+            grouped = ring.tile([P, PASS * PACK], BF16, name="wang_grouped", align_bytes=64)
+            dst = grouped[:].rearrange("p (i m j) -> p m i j", i=PACK, j=PACK)
+            src = wang_raw[b, a][:].rearrange("p j (m i) -> p m i j", i=PACK)
+            for piece in range(pieces):
+                ms = slice(piece * P // pieces, (piece + 1) * P // pieces)
+                engine_copy(dst[:, ms], src[:, ms])
+            wang_codes[b, a] = keep.tile([P, PASS], U32, name="wang_codes%d%d" % (b, a), align_bytes=64)
+            wang_scales[b, a] = keep.tile([P, PASS], U8, name="wang_scales%d%d" % (b, a), align_bytes=64)
+            nc.vector.quantize_mx(
+                out=wang_codes[b, a][:].bitcast(E4M3), scales=wang_scales[b, a][:], in_=grouped[:]
+            )
 
-        def quantize_wang(b, a, cuts):
-            codes = keep.tile([P, PASS], U32, name="wang_codes%d%d" % (b, a), align_bytes=64)
-            scales = keep.tile([P, PASS], U8, name="wang_scales%d%d" % (b, a), align_bytes=64)
-            for lo, hi in cuts:
-                nc.vector.quantize_mx(
-                    out=codes[:, lo:hi].bitcast(E4M3), scales=scales[:, lo:hi],
-                    in_=wang_grouped[b, a][:, PACK * lo : PACK * hi],
+        for a in range(2):
+            quantize_wang(0, a, nc.scalar.copy, 1)
+
+        v_scales, v_words = {}, {}
+        for a in range(2):
+            plane = keep.tile([P, S], U8, name="v_scales%d" % a, align_bytes=64)
+            nc.vector.tensor_copy(plane[:], tab_planes[:, a, :].indirect(pick[:]))
+            for h in range(2):
+                v_scales[a, h] = plane[:, h * HALF : (h + 1) * HALF]
+        for a in range(2):
+            for h in range(2):
+                v_words[a, h] = keep.tile([P, HALF], U32, name="v_words%d%d" % (a, h), align_bytes=64)
+                nc.vector.tensor_copy(
+                    v_words[a, h][:], table[a][:].bitcast(U32).indirect(entries(pick, h * HALF, HALF))
                 )
-            wang_codes[b, a], wang_scales[b, a] = codes, scales
 
         plain = {}
 
-        def plain_part(b, h, jb, on_vector=False):
-            if jb == 0:
-                plain[b, h] = ring.tile([P, BLOCKS, PACK, P], F32, name="plain", bufs=PB)
-            bank = psum.tile([P, PASS], F32, name="plain_bank")
-            cols = slice(jb * P, (jb + 1) * P)
-            for a in range(2):
-                nc.tensor.matmul_mx(
-                    out=bank[:],
-                    lhsT=v_words[a, h][:, cols].bitcast(E4M3),
-                    lhsT_scale=v_scales[a, h][:, cols],
-                    rhs=w4[b][:, a, :].bitcast(E2M1),
-                    rhs_scale=w4_planes[:, a, b * PASS : (b + 1) * PASS],
-                    start=(a == 0), stop=(a == 1),
-                )
-            dealt = bank[:].rearrange("j (p i) -> j i p", i=PACK)
-            if on_vector:
-                nc.vector.tensor_scalar(plain[b, h][:, jb], dealt, 1.0 / math.sqrt(2.0), None, ALU.mult)
-            else:
-                nc.scalar.activation(plain[b, h][:, jb], dealt, ACT.Copy, scale=1.0 / math.sqrt(2.0))
+        def plain_part(b, h, blocks, on_vector):
+            for jb in blocks:
+                if jb == 0:
+                    plain[b, h] = ring.tile([P, BLOCKS, PACK, P], F32, name="plain")
+                bank = psum.tile([P, PASS], F32, name="plain_bank")
+                cols = slice(jb * P, (jb + 1) * P)
+                for a in range(2):
+                    nc.tensor.matmul_mx(
+                        out=bank[:],
+                        lhsT=v_words[a, h][:, cols].bitcast(E4M3),
+                        lhsT_scale=v_scales[a, h][:, cols],
+                        rhs=w4[b][:, a, :].bitcast(E2M1),
+                        rhs_scale=w4_planes[:, a, b * PASS : (b + 1) * PASS],
+                        start=(a == 0), stop=(a == 1),
+                    )
+                dealt = bank[:].rearrange("j (p i) -> j i p", i=PACK)
+                if on_vector:
+                    nc.vector.tensor_scalar(plain[b, h][:, jb], dealt, 1.0 / math.sqrt(2.0), None, ALU.mult)
+                else:
+                    nc.scalar.activation(plain[b, h][:, jb], dealt, ACT.Copy, scale=1.0 / math.sqrt(2.0))
 
-        for a in range(2):
-            cast_wang(0, a, [(nc.scalar.copy, 0, P)])
-            quantize_wang(0, a, [(0, PASS)])
-        pick_columns()
+        def add_turned(into, first, second):
+            nc.tensor.matmul(into, first, ident[:], is_transpose=True, start=True, stop=False)
+            nc.tensor.matmul(into, second, ident[:], is_transpose=True, start=False, stop=True)
 
-        units = [(0, 0, 256), (0, 256, 256), (1, 0, HALF), (0, HALF, HALF), (1, HALF, HALF)]
-        units.extend((2 * pair + e, h * HALF, HALF) for pair in range(1, 4) for h in range(2) for e in range(2))
-        turns, whole, less, sines, feats, angle_banks, frac_banks, feat_banks = {}, {}, {}, {}, {}, {}, {}, {}
+        turns, less, sines = {}, {}, {}
 
-        def angle_matmul(n):
-            s, lo, width = units[n]
+        def angle(n):
+            s, lo, width = UNITS[n]
             b, i = divmod(s, PACK)
-            h, at = divmod(lo, HALF)
+            h, first = divmod(lo, HALF)
             bank = psum.tile([P, HALF], F32, name="angle_bank")
             for a in range(2):
                 nc.tensor.matmul_mx(
                     out=bank[:, :width],
                     lhsT=wang_codes[b, a][:, i * P : (i + 1) * P].bitcast(E4M3),
                     lhsT_scale=wang_scales[b, a][:, i * P : (i + 1) * P],
-                    rhs=v_words[a, h][:, at : at + width].bitcast(E4M3),
-                    rhs_scale=v_scales[a, h][:, at : at + width],
+                    rhs=v_words[a, h][:, first : first + width].bitcast(E4M3),
+                    rhs_scale=v_scales[a, h][:, first : first + width],
                     start=(a == 0), stop=(a == 1),
                 )
-            angle_banks[n] = bank
-
-        def to_turns(n):
-            s, lo, width = units[n]
-            turns[n] = ring.tile([P, HALF], F32, name="turns", bufs=TB)
+            turns[n] = ring.tile([P, HALF], F32, name="turns", bufs=3)
             nc.scalar.activation(
-                turns[n][:, :width], angle_banks[n][:, :width], ACT.Identity,
+                turns[n][:, :width], bank[:, :width], ACT.Identity,
                 bias=turns_bias[:, s : s + 1], scale=1.0 / (2 * math.pi),
             )
-
-        def to_whole(n):
-            width = units[n][2]
-            whole[n] = ring.tile([P, HALF], U32, name="whole")
-            nc.scalar.activation(whole[n][:, :width], turns[n][:, :width], ACT.Copy, bias=ROUNDER, scale=1.0)
-
-        def to_less(n):
-            width = units[n][2]
+            whole = ring.tile([P, HALF], U32, name="whole")
+            nc.scalar.activation(whole[:, :width], turns[n][:, :width], ACT.Copy, bias=ROUNDER, scale=1.0)
             less[n] = ring.tile([P, HALF], F32, name="less")
-            nc.scalar.activation(less[n][:, :width], whole[n][:, :width], ACT.Copy, bias=ROUNDER, scale=-1.0)
+            nc.scalar.activation(less[n][:, :width], whole[:, :width], ACT.Copy, bias=ROUNDER, scale=-1.0)
 
-        def add_turned(bank, width, first, second):
+        def sine(n, bank_tag):
+            width = UNITS[n][2]
+            bank = psum.tile([P, HALF], F32, name="fraction_bank", tag=bank_tag)
             for jb in range(width // P):
                 cols = slice(jb * P, (jb + 1) * P)
-                nc.tensor.matmul(bank[:, cols], first(jb), ident[:], is_transpose=True, start=True, stop=False)
-                nc.tensor.matmul(bank[:, cols], second(jb), ident[:], is_transpose=True, start=False, stop=True)
-
-        def fraction(n):
-            tag = "plain_bank" if n in FP else "frac_bank"
-            bank = psum.tile([P, HALF], F32, name="frac_bank", tag=tag)
-            add_turned(
-                bank, units[n][2],
-                lambda jb: turns[n][:, jb * P : (jb + 1) * P],
-                lambda jb: less[n][:, jb * P : (jb + 1) * P],
-            )
-            frac_banks[n] = bank
-
-        def sine(n):
-            width = units[n][2]
+                add_turned(bank[:, cols], turns[n][:, cols], less[n][:, cols])
             sines[n] = ring.tile([P, HALF], F32, name="sines")
-            nc.scalar.activation(sines[n][:, :width], frac_banks[n][:, :width], ACT.Sin, scale=2 * math.pi)
+            nc.scalar.activation(sines[n][:, :width], bank[:, :width], ACT.Sin, scale=2 * math.pi)
 
-        def feature_sum(n):
-            s, lo, width = units[n]
+        def put_features(n):
+            s, lo, width = UNITS[n]
             b, i = divmod(s, PACK)
-            h, at = divmod(lo, HALF)
-            bank = psum.tile([P, HALF], F32, name="feat_bank")
-            add_turned(
-                bank, width,
-                lambda jb: plain[b, h][:, at // P + jb, i, :],
-                lambda jb: sines[n][:, jb * P : (jb + 1) * P],
-            )
-            feat_banks[n] = bank
-
-        def feature(n):
-            s, lo, width = units[n]
-            feats[n] = ring.tile([P, HALF], F32, name="feats", bufs=FB)
-            nc.scalar.activation(
-                feats[n][:, :width], feat_banks[n][:, :width], ACT.Copy, scale=gain_root2[:, s : s + 1]
-            )
-
-        def store_in_page(n):
-            s, lo, width = units[n]
+            h, first = divmod(lo, HALF)
+            bank = psum.tile([P, HALF], F32, name="feature_bank")
+            for jb in range(width // P):
+                cols = slice(jb * P, (jb + 1) * P)
+                add_turned(bank[:, cols], plain[b, h][:, first // P + jb, i, :], sines[n][:, cols])
+            features = ring.tile([P, HALF], F32, name="features", bufs=3)
+            nc.scalar.activation(features[:, :width], bank[:, :width], ACT.Copy, scale=gain_root2[:, s : s + 1])
             nc.vector.tensor_tensor(
                 pages[s % 2][:].indirect(entries(put, lo, width)),
-                feats[n][:, :width], put_weight[:, lo : lo + width], ALU.mult,
+                features[:, :width], put_weight[:, lo : lo + width], ALU.mult,
             )
 
-        routine, offsets_of, woven, z_codes, z_scales = {}, {}, {}, {}, {}
+        minus_read_weight = keep.tile([P, M], F32, name="minus_read_weight")
+        routine, exec_offsets, woven, z_codes, z_scales, turned_pairs = {}, {}, {}, {}, {}, {}
+
+        def negate_read_weight():
+            nc.scalar.activation(minus_read_weight[:], read_weight[:], ACT.Copy, scale=-1.0)
 
         def read_page(s, lo, width):
             b, i = divmod(s, PACK)
@@ -282,23 +254,17 @@ def tile_list_flight_shape_scores_kernel(
             nc.vector.tensor_tensor(
                 routine[b][:, i, lo : lo + width],
                 pages[s % 2][:].indirect(entries(read, lo, width)),
-                read_weight[:, lo : lo + width], ALU.mult,
+                (minus_read_weight if b == 0 else read_weight)[:, lo : lo + width], ALU.mult,
             )
 
         def load_execm(b):
-            offsets_of[b] = ring.tile([P, PACK, M], F32, name="exec_offsets", tag="wide")
+            exec_offsets[b] = ring.tile([P, PACK, M], F32, name="exec_offsets", tag="wide")
             nc.sync.dma_start(
-                offsets_of[b][:], execm[b * PASS : (b + 1) * PASS, :].rearrange("(p i) m -> p i m", i=PACK)
+                exec_offsets[b][:], execm[b * PASS : (b + 1) * PASS, :].rearrange("(p i) m -> p i m", i=PACK)
             )
 
-        def subtract(b, lo, width):
-            woven[b, lo] = ring.tile([P, width * PACK], BF16, name="woven", tag="grouped", align_bytes=64)
-            nc.vector.tensor_tensor(
-                woven[b, lo][:].rearrange("p (c w i) -> p c i w", w=2, i=PACK),
-                routine[b][:, :, lo : lo + width].rearrange("p i (c w) -> p c i w", w=2),
-                offsets_of[b][:, :, lo : lo + width].rearrange("p i (c w) -> p c i w", w=2),
-                ALU.subtract,
-            )
+        def new_woven(b, lo, width):
+            woven[b, lo] = ring.tile([P, width * PACK], BF16, name="woven", bufs=3, align_bytes=64)
 
         def quantize_z(b, lo, width):
             if lo == 0:
@@ -307,6 +273,48 @@ def tile_list_flight_shape_scores_kernel(
             nc.vector.quantize_mx(
                 out=z_codes[b][:, lo : lo + width].bitcast(E4M3), scales=z_scales[b][:, lo : lo + width],
                 in_=woven[b, lo][:],
+            )
+
+        def first_rows_z(q):
+            for u in range(2):
+                bank = psum.tile([P, 2, QUARTER], F32, name="difference_bank", tag="plain_bank")
+                for e in range(2):
+                    for mb in range(2):
+                        cols = slice(q * QUARTER + mb * P, q * QUARTER + (mb + 1) * P)
+                        add_turned(
+                            bank[:, e, mb * P : (mb + 1) * P],
+                            routine[0][:, 2 * u + e, cols], exec_offsets[0][:, 2 * u + e, cols],
+                        )
+                turned_pairs[u] = ring.tile([P, 2 * QUARTER], BF16, name="turned_pairs", bufs=4)
+                nc.scalar.activation(
+                    turned_pairs[u][:].rearrange("m (c w e) -> m c e w", w=4, e=2),
+                    bank[:].rearrange("m e (c w) -> m c e w", w=4),
+                    ACT.Copy, scale=-1.0,
+                )
+            h, part = divmod(q, 2)
+            if part == 0:
+                new_woven(0, h * HALF, HALF)
+            bank = psum.tile([P, 2, QUARTER], F32, name="words_bank", tag="plain_bank")
+            for u in range(2):
+                words = turned_pairs[u][:].bitcast(F32)
+                for mb in range(2):
+                    cols = slice(mb * P, (mb + 1) * P)
+                    nc.tensor.transpose(bank[:, u, cols], words[:, cols], ident[:])
+            nc.scalar.copy(
+                woven[0, h * HALF][:].bitcast(F32)[:, part * HALF : (part + 1) * HALF]
+                .rearrange("p (c w u) -> p c u w", w=2, u=2),
+                bank[:].rearrange("p u (c w) -> p c u w", w=2),
+            )
+            if part == 1:
+                quantize_z(0, h * HALF, HALF)
+
+        def last_rows_z(lo, width):
+            new_woven(1, lo, width)
+            nc.vector.tensor_tensor(
+                woven[1, lo][:].rearrange("p (c w i) -> p c i w", w=2, i=PACK),
+                routine[1][:, :, lo : lo + width].rearrange("p i (c w) -> p c i w", w=2),
+                exec_offsets[1][:, :, lo : lo + width].rearrange("p i (c w) -> p c i w", w=2),
+                ALU.subtract,
             )
 
         form_grouped = keep.tile([P, 2, N, PACK], BF16, name="form_grouped", align_bytes=64)
@@ -320,8 +328,8 @@ def tile_list_flight_shape_scores_kernel(
                 form_raw[b][:], wform[b * PASS : (b + 1) * PASS, :].rearrange("(p i) n -> p i n", i=PACK)
             )
 
-        def cast_form(b):
-            for nt in range(3):
+        def round_form(b):
+            for nt in range(SCORE_TILES):
                 cols = slice(nt * P, (nt + 1) * P)
                 nc.scalar.copy(
                     form_grouped[:, b, cols].rearrange("p (c w) i -> p c i w", w=2),
@@ -330,42 +338,44 @@ def tile_list_flight_shape_scores_kernel(
 
         def quantize_form():
             flat = form_grouped[:].rearrange("p b n i -> p (b n i)")
-            for lo, hi in ((0, 512), (512, 768)):
+            for lo, hi in ((0, PASS), (PASS, 2 * N)):
                 nc.vector.quantize_mx(
                     out=form_codes[:, lo:hi].bitcast(E4M3), scales=form_scales[:, lo:hi],
                     in_=flat[:, PACK * lo : PACK * hi],
                 )
 
         score_banks = {}
-        free_tags = ["angle_bank", "angle_bank", "frac_bank", "frac_bank", "plain_bank", "plain_bank",
-                     "feat_bank", "feat_bank"]
+        score_tags = [tag for tag in ("angle_bank", "fraction_bank", "plain_bank", "feature_bank") for buf in range(2)]
 
         def score_passes(b, c):
-            lo, width = chunks[c]
+            lo, width = CHUNKS[c]
             share = HALF // width
-            for nt in range(3):
-                k, place = divmod(nt, share)
+            for nt in range(SCORE_TILES):
+                which, place = divmod(nt, share)
                 if b == 0 and place == 0:
-                    bank = psum.tile([P, HALF], F32, name="score_bank", tag=free_tags[len(score_banks)])
-                    score_banks[c, k] = bank
+                    bank = psum.tile([P, HALF], F32, name="score_bank", tag=score_tags[len(score_banks)])
+                    score_banks[c, which] = bank
                 cols = slice(b * N + nt * P, b * N + (nt + 1) * P)
                 nc.tensor.matmul_mx(
-                    out=score_banks[c, k][:, place * width : (place + 1) * width],
+                    out=score_banks[c, which][:, place * width : (place + 1) * width],
                     lhsT=form_codes[:, cols].bitcast(E4M3), lhsT_scale=form_scales[:, cols],
                     rhs=z_codes[b][:, lo : lo + width].bitcast(E4M3), rhs_scale=z_scales[b][:, lo : lo + width],
-                    start=(b == 0 and place == 0), stop=(b == 1 and (nt == 2 or place == share - 1)),
+                    start=(b == 0 and place == 0),
+                    stop=(b == 1 and (nt == SCORE_TILES - 1 or place == share - 1)),
                 )
 
-        def store_scores(c, engine_copy):
-            lo, width = chunks[c]
+        def finish_chunk(c, engine_copy):
+            lo, width = CHUNKS[c]
             share = HALF // width
+            quantize_z(1, lo, width)
             score_passes(1, c)
-            scores = ring.tile([P, 3, width], F32, name="scores", tag="raw" if c < 3 else "plain", bufs=3 if c < 3 else PB)
-            for first in range(0, 3, share):
-                last = min(first + share, 3)
+            tag, bufs = ("raw", 3) if c < 3 else ("plain", 2)
+            scores = ring.tile([P, SCORE_TILES, width], F32, name="scores", tag=tag, bufs=bufs)
+            for first in range(0, SCORE_TILES, share):
+                end = min(first + share, SCORE_TILES)
                 engine_copy(
-                    scores[:, first:last, :].rearrange("p t m -> p (t m)"),
-                    score_banks[c, first // share][:, : (last - first) * width],
+                    scores[:, first:end, :].rearrange("p t m -> p (t m)"),
+                    score_banks[c, first // share][:, : (end - first) * width],
                 )
             nc.sync.dma_start(out[:, lo : lo + width].rearrange("(t p) m -> p t m", p=P), scores[:])
 
@@ -374,95 +384,46 @@ def tile_list_flight_shape_scores_kernel(
         load_form(1)
         load_execm(1)
 
-        chunks = [(0, 256), (256, 256), (512, 256), (768, P), (896, P)]
+        behind = {}
 
-        extra = {}
+        def after(n, job, *args):
+            behind.setdefault(n, []).append((job, args))
 
-        def at(step, job, *args):
-            extra.setdefault(step, []).append((job, args))
-
-        before_sum = {3: [(plain_part, (0, 1, jb)) for jb in range(BLOCKS)]}
-        for jb in range(BLOCKS):
-            at(P0 + jb // 2, plain_part, 1, 0, jb)
-            at(P1 + jb // 2, plain_part, 1, 1, jb)
+        plain_from = [1 + last_unit_where(lambda s, lo, width: s < PACK and lo // HALF == h) for h in range(2)]
+        for two in range(2):
+            for h in range(2):
+                after(plain_from[h] + two, plain_part, 1, h, (2 * two, 2 * two + 1), False)
         for a in range(2):
-            at(CW + a, cast_wang, 1, a, [(nc.vector.tensor_copy if CV else nc.scalar.copy, 32 * c, 32 * c + 32) for c in range(4)])
-            at(CW + a, quantize_wang, 1, a, [(0, PASS)])
-            at(10 + a, cast_form, a)
-        at(11, quantize_form)
-        for s in range(7):
-            last = 4 * (s // 2) + 3 + s % 2
-            at(last, read_page, s, 0, M)
-        for h in range(2):
-            at(8, subtract, 0, h * HALF, HALF)
-        for h in range(2):
-            at(8, quantize_z, 0, h * HALF, HALF)
+            after(WANG_UNIT + a, quantize_wang, 1, a, nc.vector.tensor_copy, 4)
+            after(FORM_UNIT + a, round_form, a)
+        after(FORM_UNIT + 1, quantize_form)
+        page_done = [last_unit_where(lambda s, lo, width: s == page_slice) for page_slice in range(SLICES)]
+        after(page_done[0] - 1, negate_read_weight)
+        for s in range(SLICES - 1):
+            after(page_done[s], read_page, s, 0, M)
+        z_from = plain_from[1] + 2
+        for q in range(M // QUARTER):
+            after(min(z_from + 2 * q, LAST_UNIT), first_rows_z, q)
 
-        def reduce_angle(n):
-            angle_matmul(n)
-            to_turns(n)
-            to_whole(n)
-            if n in DIRECT:
-                fraction_direct(n)
-            else:
-                to_less(n)
-
-        def fraction_direct(n):
-            width = units[n][2]
-            less[n] = ring.tile([P, HALF], F32, name="less")
-            nc.vector.scalar_tensor_tensor(
-                less[n][:, :width], whole[n][:, :width].bitcast(I32), ROUNDER, turns[n][:, :width],
-                ALU.subtract, ALU.subtract,
-            )
-
-        def feature_direct(n):
-            s, lo, width = units[n]
-            b, i = divmod(s, PACK)
-            h, at_col = divmod(lo, HALF)
-            sines[n] = ring.tile([P, HALF], F32, name="sines")
-            nc.scalar.activation(sines[n][:, :width], less[n][:, :width], ACT.Sin, scale=-2 * math.pi)
-            for job, args in before_sum.get(n, []):
-                job(*args)
-            bank = psum.tile([P, HALF], F32, name="feat_bank")
-            for jb in range(width // P):
-                nc.tensor.transpose(bank[:, jb * P : (jb + 1) * P], plain[b, h][:, at_col // P + jb, i, :], ident[:])
-            gained = ring.tile([P, HALF], F32, name="gained")
-            nc.scalar.activation(gained[:, :width], bank[:, :width], ACT.Copy, scale=gain_root2[:, s : s + 1])
-            feats[n] = ring.tile([P, HALF], F32, name="feats", bufs=FB)
-            nc.vector.scalar_tensor_tensor(
-                feats[n][:, :width], sines[n][:, :width], gain_root2[:, s : s + 1], gained[:, :width],
-                ALU.mult, ALU.add,
-            )
-
-        AHEAD = 3
-        for n in range(AHEAD):
-            reduce_angle(n)
-        for jb in range(BLOCKS):
-            plain_part(0, 0, jb, True)
-        count = len(units)
-        for n in range(count):
-            if n >= AHEAD:
-                reduce_angle(n)
-            if n in DIRECT:
-                feature_direct(n)
-            else:
-                fraction(n)
-                sine(n)
-                for job, args in before_sum.get(n, []):
-                    job(*args)
-                feature_sum(n)
-                feature(n)
-            store_in_page(n)
-            for job, args in extra.get(n, []):
+        first_of_second_half = min(n for n, unit in enumerate(UNITS) if unit[1] >= HALF)
+        for n in range(ANGLES_AHEAD):
+            angle(n)
+        plain_part(0, 0, range(BLOCKS), True)
+        for n in range(len(UNITS)):
+            if n >= ANGLES_AHEAD:
+                angle(n)
+            sine(n, "plain_bank" if n in (z_from - 1, z_from) else "fraction_bank")
+            if n == first_of_second_half:
+                plain_part(0, 1, range(BLOCKS), False)
+            put_features(n)
+            for job, args in behind.get(n, []):
                 job(*args)
 
-        for c in range(len(chunks)):
+        for c in range(len(CHUNKS)):
             score_passes(0, c)
-        for c, (lo, width) in enumerate(chunks):
-            read_page(7, lo, width)
+        for c, (lo, width) in enumerate(CHUNKS):
+            read_page(SLICES - 1, lo, width)
             if c > 0:
-                quantize_z(1, *chunks[c - 1])
-                store_scores(c - 1, nc.scalar.copy)
-            subtract(1, lo, width)
-        quantize_z(1, *chunks[-1])
-        store_scores(len(chunks) - 1, nc.vector.tensor_copy)
+                finish_chunk(c - 1, nc.scalar.copy)
+            last_rows_z(lo, width)
+        finish_chunk(len(CHUNKS) - 1, nc.vector.tensor_copy)

import math
from contextlib import ExitStack

import concourse.mybir as mybir
from concourse.masks import make_identity

K, H, N, T, S, M, T2 = 1024, 1024, 384, 4096, 1024, 1024, 2048
FLOPS = 2 * (2 * K * H * S + H * N * M)

F32 = mybir.dt.float32
BF16 = mybir.dt.bfloat16
I32 = mybir.dt.int32
U32 = mybir.dt.uint32
U16 = mybir.dt.uint16
U8 = mybir.dt.uint8
E4M3 = mybir.dt.float8_e4m3fn_x4
E2M1 = mybir.dt.float4_e2m1fn_x4
ALU = mybir.AluOpType
ACT = mybir.ActivationFunctionType

P = 128
PACK = 4
PASS = P * PACK
HALF = 512
QUARTER = HALF // 2
BLOCKS = HALF // P
SLICES = H // P
SCORE_TILES = N // P
ROUNDER = 1.5 * 2.0 ** 23

UNITS = [(0, 0, QUARTER), (0, QUARTER, QUARTER), (1, 0, HALF), (0, HALF, HALF), (1, HALF, HALF)] + [
    (2 * pair + e, h * HALF, HALF) for pair in range(1, SLICES // 2) for h in range(2) for e in range(2)
]
LAST_UNIT = len(UNITS) - 1
ANGLES_AHEAD = 3
WANG_UNIT, FORM_UNIT = 3, 10
CHUNKS = [(0, QUARTER), (QUARTER, QUARTER), (HALF, QUARTER), (HALF + QUARTER, P), (M - P, P)]


def last_unit_where(wanted):
    return max(n for n, unit in enumerate(UNITS) if wanted(*unit))


def tile_list_flight_shape_scores_kernel(
    tc, tab_words, tab_scales, offs, offs2, offs3, w4_words, w4_scales,
    wang, tilt, gain, wgs, wgt, execm, wform, out,
):
    nc = tc.nc
    with ExitStack() as ctx:
        lists = ctx.enter_context(tc.tile_pool(name="lists", bufs=1))
        keep = ctx.enter_context(tc.tile_pool(name="keep", bufs=1))
        ring = ctx.enter_context(tc.tile_pool(name="ring", bufs=2))
        psum = ctx.enter_context(tc.psum_pool(name="psum", bufs=2))

        pick = lists.tile([P, S // 16], U16, name="pick")
        put = lists.tile([P, S // 16], U16, name="put")
        read = lists.tile([P, M // 16], U16, name="read")

        def entries(offsets, lo, width):
            return offsets[:, lo // 16 : (lo + width) // 16]

        tab_planes = ring.tile([P, 2, T], U8, name="tab_planes", tag="routine")
        w4_planes = keep.tile([P, 2, H], U8, name="w4_planes", align_bytes=64)
        nc.vector.memset(tab_planes[:, 0, :].bitcast(I32), 0)
        nc.gpsimd.memset(tab_planes[:, 1, :].bitcast(I32), 0)
        nc.gpsimd.memset(w4_planes[:].bitcast(I32), 0)
        pages = []
        for g in range(2):
            page = keep.tile([P, T2], F32, name="page%d" % g)
            nc.vector.memset(page[:], 0.0)
            pages.append(page)
        one = keep.tile([P, 1], F32, name="one")
        nc.gpsimd.memset(one[:], 1.0)
        sine_eighth = keep.tile([P, 1], F32, name="sine_eighth")
        nc.scalar.activation(sine_eighth[:], one[:], ACT.Sin, scale=math.pi / 4)

        table, wang_raw, w4 = {}, {}, {}

        def load_table(a):
            table[a] = ring.tile([P, T], I32, name="table", tag="wide")
            nc.sync.dma_start(table[a][:], tab_words[a].rearrange("p t i -> p (t i)").bitcast(I32))

        def load_wang(b, a):
            wang_raw[b, a] = ring.tile([P, PACK, PASS], F32, name="wang_raw", tag="raw", bufs=3)
            rows = wang[a * PASS : (a + 1) * PASS, b * PASS : (b + 1) * PASS]
            nc.sync.dma_start(wang_raw[b, a][:], rows.rearrange("(p j) c -> p j c", j=PACK))

        def load_w4(b):
            w4[b] = keep.tile([P, 2, 2 * PASS], U8, name="w4_%d" % b, align_bytes=64)
            nc.sync.dma_start(
                w4[b][:].bitcast(I32),
                w4_words[:, :, 2 * b * PASS : 2 * (b + 1) * PASS].rearrange("a p c -> p a c").bitcast(I32),
            )

        def load_planes(planes, scale_rows):
            for r in range(4):
                nc.sync.dma_start(
                    planes[r:P:32].bitcast(I32),
                    scale_rows[:, r:16:4, :].rearrange("a q c -> q a c").bitcast(I32),
                )

        nc.sync.dma_start(pick[:], offs)
        load_table(0)
        load_planes(tab_planes, tab_scales)
        for a in range(2):
            load_wang(0, a)
        row_tilt = keep.tile([P, 2, PACK], F32, name="row_tilt")
        row_gain = keep.tile([P, 2, PACK], F32, name="row_gain")
        nc.sync.dma_start(row_tilt[:], tilt.rearrange("(b p i) -> p b i", b=2, i=PACK))
        nc.sync.dma_start(row_gain[:], gain.rearrange("(b p i) -> p b i", b=2, i=PACK))
        load_w4(0)
        load_table(1)
        load_planes(w4_planes, w4_scales)
        put_weight = keep.tile([P, S], F32, name="put_weight")
        nc.sync.dma_start(put_weight[:], wgs)
        nc.sync.dma_start(put[:], offs2)
        for a in range(2):
            load_wang(1, a)
        nc.sync.dma_start(read[:], offs3)
        read_weight = keep.tile([P, M], F32, name="read_weight")
        nc.sync.dma_start(read_weight[:], wgt)
        load_w4(1)
        ident = keep.tile([P, P], F32, name="ident")
        make_identity(nc, ident[:])

        turns_bias = keep.tile([P, SLICES], F32, name="turns_bias")
        nc.scalar.activation(
            turns_bias[:], row_tilt[:].rearrange("p b i -> p (b i)"), ACT.Copy,
            bias=-1.0 / 8, scale=1.0 / (2 * math.pi),
        )
        gain_root2 = keep.tile([P, SLICES], F32, name="gain_root2")
        nc.vector.tensor_scalar(
            gain_root2[:], row_gain[:].rearrange("p b i -> p (b i)"), sine_eighth[:], 2.0, ALU.mult, ALU.mult
        )

        wang_codes, wang_scales = {}, {}

        def quantize_wang(b, a, engine_copy, pieces):
            grouped = ring.tile([P, PASS * PACK], BF16, name="wang_grouped", align_bytes=64)
            dst = grouped[:].rearrange("p (i m j) -> p m i j", i=PACK, j=PACK)
            src = wang_raw[b, a][:].rearrange("p j (m i) -> p m i j", i=PACK)
            for piece in range(pieces):
                ms = slice(piece * P // pieces, (piece + 1) * P // pieces)
                engine_copy(dst[:, ms], src[:, ms])
            wang_codes[b, a] = keep.tile([P, PASS], U32, name="wang_codes%d%d" % (b, a), align_bytes=64)
            wang_scales[b, a] = keep.tile([P, PASS], U8, name="wang_scales%d%d" % (b, a), align_bytes=64)
            nc.vector.quantize_mx(
                out=wang_codes[b, a][:].bitcast(E4M3), scales=wang_scales[b, a][:], in_=grouped[:]
            )

        for a in range(2):
            quantize_wang(0, a, nc.scalar.copy, 1)

        v_scales, v_words = {}, {}
        for a in range(2):
            plane = keep.tile([P, S], U8, name="v_scales%d" % a, align_bytes=64)
            nc.vector.tensor_copy(plane[:], tab_planes[:, a, :].indirect(pick[:]))
            for h in range(2):
                v_scales[a, h] = plane[:, h * HALF : (h + 1) * HALF]
        for a in range(2):
            for h in range(2):
                v_words[a, h] = keep.tile([P, HALF], U32, name="v_words%d%d" % (a, h), align_bytes=64)
                nc.vector.tensor_copy(
                    v_words[a, h][:], table[a][:].bitcast(U32).indirect(entries(pick, h * HALF, HALF))
                )

        plain = {}

        def plain_part(b, h, blocks, on_vector):
            for jb in blocks:
                if jb == 0:
                    plain[b, h] = ring.tile([P, BLOCKS, PACK, P], F32, name="plain")
                bank = psum.tile([P, PASS], F32, name="plain_bank")
                cols = slice(jb * P, (jb + 1) * P)
                for a in range(2):
                    nc.tensor.matmul_mx(
                        out=bank[:],
                        lhsT=v_words[a, h][:, cols].bitcast(E4M3),
                        lhsT_scale=v_scales[a, h][:, cols],
                        rhs=w4[b][:, a, :].bitcast(E2M1),
                        rhs_scale=w4_planes[:, a, b * PASS : (b + 1) * PASS],
                        start=(a == 0), stop=(a == 1),
                    )
                dealt = bank[:].rearrange("j (p i) -> j i p", i=PACK)
                if on_vector:
                    nc.vector.tensor_scalar(plain[b, h][:, jb], dealt, 1.0 / math.sqrt(2.0), None, ALU.mult)
                else:
                    nc.scalar.activation(plain[b, h][:, jb], dealt, ACT.Copy, scale=1.0 / math.sqrt(2.0))

        def add_turned(into, first, second):
            nc.tensor.matmul(into, first, ident[:], is_transpose=True, start=True, stop=False)
            nc.tensor.matmul(into, second, ident[:], is_transpose=True, start=False, stop=True)

        turns, less, sines = {}, {}, {}

        def angle(n):
            s, lo, width = UNITS[n]
            b, i = divmod(s, PACK)
            h, first = divmod(lo, HALF)
            bank = psum.tile([P, HALF], F32, name="angle_bank")
            for a in range(2):
                nc.tensor.matmul_mx(
                    out=bank[:, :width],
                    lhsT=wang_codes[b, a][:, i * P : (i + 1) * P].bitcast(E4M3),
                    lhsT_scale=wang_scales[b, a][:, i * P : (i + 1) * P],
                    rhs=v_words[a, h][:, first : first + width].bitcast(E4M3),
                    rhs_scale=v_scales[a, h][:, first : first + width],
                    start=(a == 0), stop=(a == 1),
                )
            turns[n] = ring.tile([P, HALF], F32, name="turns", bufs=3)
            nc.scalar.activation(
                turns[n][:, :width], bank[:, :width], ACT.Identity,
                bias=turns_bias[:, s : s + 1], scale=1.0 / (2 * math.pi),
            )
            whole = ring.tile([P, HALF], U32, name="whole")
            nc.scalar.activation(whole[:, :width], turns[n][:, :width], ACT.Copy, bias=ROUNDER, scale=1.0)
            less[n] = ring.tile([P, HALF], F32, name="less")
            nc.scalar.activation(less[n][:, :width], whole[:, :width], ACT.Copy, bias=ROUNDER, scale=-1.0)

        def sine(n, bank_tag):
            width = UNITS[n][2]
            bank = psum.tile([P, HALF], F32, name="fraction_bank", tag=bank_tag)
            for jb in range(width // P):
                cols = slice(jb * P, (jb + 1) * P)
                add_turned(bank[:, cols], turns[n][:, cols], less[n][:, cols])
            sines[n] = ring.tile([P, HALF], F32, name="sines")
            nc.scalar.activation(sines[n][:, :width], bank[:, :width], ACT.Sin, scale=2 * math.pi)

        def put_features(n):
            s, lo, width = UNITS[n]
            b, i = divmod(s, PACK)
            h, first = divmod(lo, HALF)
            bank = psum.tile([P, HALF], F32, name="feature_bank")
            for jb in range(width // P):
                cols = slice(jb * P, (jb + 1) * P)
                add_turned(bank[:, cols], plain[b, h][:, first // P + jb, i, :], sines[n][:, cols])
            features = ring.tile([P, HALF], F32, name="features", bufs=3)
            nc.scalar.activation(features[:, :width], bank[:, :width], ACT.Copy, scale=gain_root2[:, s : s + 1])
            nc.vector.tensor_tensor(
                pages[s % 2][:].indirect(entries(put, lo, width)),
                features[:, :width], put_weight[:, lo : lo + width], ALU.mult,
            )

        minus_read_weight = keep.tile([P, M], F32, name="minus_read_weight")
        routine, exec_offsets, woven, z_codes, z_scales, turned_pairs = {}, {}, {}, {}, {}, {}

        def negate_read_weight():
            nc.scalar.activation(minus_read_weight[:], read_weight[:], ACT.Copy, scale=-1.0)

        def read_page(s, lo, width):
            b, i = divmod(s, PACK)
            if i == 0:
                routine[b] = ring.tile([P, PACK, M], F32, name="routine")
            nc.vector.tensor_tensor(
                routine[b][:, i, lo : lo + width],
                pages[s % 2][:].indirect(entries(read, lo, width)),
                (minus_read_weight if b == 0 else read_weight)[:, lo : lo + width], ALU.mult,
            )

        def load_execm(b):
            exec_offsets[b] = ring.tile([P, PACK, M], F32, name="exec_offsets", tag="wide")
            nc.sync.dma_start(
                exec_offsets[b][:], execm[b * PASS : (b + 1) * PASS, :].rearrange("(p i) m -> p i m", i=PACK)
            )

        def new_woven(b, lo, width):
            woven[b, lo] = ring.tile([P, width * PACK], BF16, name="woven", bufs=3, align_bytes=64)

        def quantize_z(b, lo, width):
            if lo == 0:
                z_codes[b] = keep.tile([P, M], U32, name="z_codes%d" % b, align_bytes=64)
                z_scales[b] = keep.tile([P, M], U8, name="z_scales%d" % b, align_bytes=64)
            nc.vector.quantize_mx(
                out=z_codes[b][:, lo : lo + width].bitcast(E4M3), scales=z_scales[b][:, lo : lo + width],
                in_=woven[b, lo][:],
            )

        def first_rows_z(q):
            for u in range(2):
                bank = psum.tile([P, 2, QUARTER], F32, name="difference_bank", tag="plain_bank")
                for e in range(2):
                    for mb in range(2):
                        cols = slice(q * QUARTER + mb * P, q * QUARTER + (mb + 1) * P)
                        add_turned(
                            bank[:, e, mb * P : (mb + 1) * P],
                            routine[0][:, 2 * u + e, cols], exec_offsets[0][:, 2 * u + e, cols],
                        )
                turned_pairs[u] = ring.tile([P, 2 * QUARTER], BF16, name="turned_pairs", bufs=4)
                nc.scalar.activation(
                    turned_pairs[u][:].rearrange("m (c w e) -> m c e w", w=4, e=2),
                    bank[:].rearrange("m e (c w) -> m c e w", w=4),
                    ACT.Copy, scale=-1.0,
                )
            h, part = divmod(q, 2)
            if part == 0:
                new_woven(0, h * HALF, HALF)
            bank = psum.tile([P, 2, QUARTER], F32, name="words_bank", tag="plain_bank")
            for u in range(2):
                words = turned_pairs[u][:].bitcast(F32)
                for mb in range(2):
                    cols = slice(mb * P, (mb + 1) * P)
                    nc.tensor.transpose(bank[:, u, cols], words[:, cols], ident[:])
            nc.scalar.copy(
                woven[0, h * HALF][:].bitcast(F32)[:, part * HALF : (part + 1) * HALF]
                .rearrange("p (c w u) -> p c u w", w=2, u=2),
                bank[:].rearrange("p u (c w) -> p c u w", w=2),
            )
            if part == 1:
                quantize_z(0, h * HALF, HALF)

        def last_rows_z(lo, width):
            new_woven(1, lo, width)
            nc.vector.tensor_tensor(
                woven[1, lo][:].rearrange("p (c w i) -> p c i w", w=2, i=PACK),
                routine[1][:, :, lo : lo + width].rearrange("p i (c w) -> p c i w", w=2),
                exec_offsets[1][:, :, lo : lo + width].rearrange("p i (c w) -> p c i w", w=2),
                ALU.subtract,
            )

        form_grouped = keep.tile([P, 2, N, PACK], BF16, name="form_grouped", align_bytes=64)
        form_codes = keep.tile([P, 2 * N], U32, name="form_codes", align_bytes=64)
        form_scales = keep.tile([P, 2 * N], U8, name="form_scales", align_bytes=64)
        form_raw = {}

        def load_form(b):
            form_raw[b] = ring.tile([P, PACK, N], F32, name="form_raw", tag="raw", bufs=3)
            nc.sync.dma_start(
                form_raw[b][:], wform[b * PASS : (b + 1) * PASS, :].rearrange("(p i) n -> p i n", i=PACK)
            )

        def round_form(b):
            for nt in range(SCORE_TILES):
                cols = slice(nt * P, (nt + 1) * P)
                nc.scalar.copy(
                    form_grouped[:, b, cols].rearrange("p (c w) i -> p c i w", w=2),
                    form_raw[b][:, :, cols].rearrange("p i (c w) -> p c i w", w=2),
                )

        def quantize_form():
            flat = form_grouped[:].rearrange("p b n i -> p (b n i)")
            for lo, hi in ((0, PASS), (PASS, 2 * N)):
                nc.vector.quantize_mx(
                    out=form_codes[:, lo:hi].bitcast(E4M3), scales=form_scales[:, lo:hi],
                    in_=flat[:, PACK * lo : PACK * hi],
                )

        score_banks = {}
        score_tags = [tag for tag in ("angle_bank", "fraction_bank", "plain_bank", "feature_bank") for buf in range(2)]

        def score_passes(b, c):
            lo, width = CHUNKS[c]
            share = HALF // width
            for nt in range(SCORE_TILES):
                which, place = divmod(nt, share)
                if b == 0 and place == 0:
                    bank = psum.tile([P, HALF], F32, name="score_bank", tag=score_tags[len(score_banks)])
                    score_banks[c, which] = bank
                cols = slice(b * N + nt * P, b * N + (nt + 1) * P)
                nc.tensor.matmul_mx(
                    out=score_banks[c, which][:, place * width : (place + 1) * width],
                    lhsT=form_codes[:, cols].bitcast(E4M3), lhsT_scale=form_scales[:, cols],
                    rhs=z_codes[b][:, lo : lo + width].bitcast(E4M3), rhs_scale=z_scales[b][:, lo : lo + width],
                    start=(b == 0 and place == 0),
                    stop=(b == 1 and (nt == SCORE_TILES - 1 or place == share - 1)),
                )

        def finish_chunk(c, engine_copy):
            lo, width = CHUNKS[c]
            share = HALF // width
            quantize_z(1, lo, width)
            score_passes(1, c)
            tag, bufs = ("raw", 3) if c < 3 else ("plain", 2)
            scores = ring.tile([P, SCORE_TILES, width], F32, name="scores", tag=tag, bufs=bufs)
            for first in range(0, SCORE_TILES, share):
                end = min(first + share, SCORE_TILES)
                engine_copy(
                    scores[:, first:end, :].rearrange("p t m -> p (t m)"),
                    score_banks[c, first // share][:, : (end - first) * width],
                )
            nc.sync.dma_start(out[:, lo : lo + width].rearrange("(t p) m -> p t m", p=P), scores[:])

        load_execm(0)
        load_form(0)
        load_form(1)
        load_execm(1)

        behind = {}

        def after(n, job, *args):
            behind.setdefault(n, []).append((job, args))

        plain_from = [1 + last_unit_where(lambda s, lo, width: s < PACK and lo // HALF == h) for h in range(2)]
        for two in range(2):
            for h in range(2):
                after(plain_from[h] + two, plain_part, 1, h, (2 * two, 2 * two + 1), False)
        for a in range(2):
            after(WANG_UNIT + a, quantize_wang, 1, a, nc.vector.tensor_copy, 4)
            after(FORM_UNIT + a, round_form, a)
        after(FORM_UNIT + 1, quantize_form)
        page_done = [last_unit_where(lambda s, lo, width: s == page_slice) for page_slice in range(SLICES)]
        after(page_done[0] - 1, negate_read_weight)
        for s in range(SLICES - 1):
            after(page_done[s], read_page, s, 0, M)
        z_from = plain_from[1] + 2
        for q in range(M // QUARTER):
            after(min(z_from + 2 * q, LAST_UNIT), first_rows_z, q)

        first_of_second_half = min(n for n, unit in enumerate(UNITS) if unit[1] >= HALF)
        for n in range(ANGLES_AHEAD):
            angle(n)
        plain_part(0, 0, range(BLOCKS), True)
        for n in range(len(UNITS)):
            if n >= ANGLES_AHEAD:
                angle(n)
            sine(n, "plain_bank" if n in (z_from - 1, z_from) else "fraction_bank")
            if n == first_of_second_half:
                plain_part(0, 1, range(BLOCKS), False)
            put_features(n)
            for job, args in behind.get(n, []):
                job(*args)

        for c in range(len(CHUNKS)):
            score_passes(0, c)
        for c, (lo, width) in enumerate(CHUNKS):
            read_page(SLICES - 1, lo, width)
            if c > 0:
                finish_chunk(c - 1, nc.scalar.copy)
            last_rows_z(lo, width)
        finish_chunk(len(CHUNKS) - 1, nc.vector.tensor_copy)
